import numpy as np
import ml_dtypes


def mxq(x, axis, fmt="e4m3"):
    dtype, down = {"e4m3": (ml_dtypes.float8_e4m3fn, 7), "e5m2": (ml_dtypes.float8_e5m2, 14)}[fmt]
    v = np.moveaxis(np.asarray(x, np.float32).astype(ml_dtypes.bfloat16).astype(np.float64), axis, -1)
    blocks = v.reshape(v.shape[:-1] + (-1, 32))
    amax = np.abs(blocks).max(-1, keepdims=True)
    byte = np.maximum(np.where(amax > 0, np.frexp(amax)[1] - 1 + 127, 0) - down, 1)
    scale = np.exp2(byte - 127.0)
    codes = (blocks / scale).astype(np.float32).astype(dtype).astype(np.float64)
    return np.moveaxis((codes * scale).reshape(v.shape), -1, axis)


WIDE = False


def mx_kscale(k):
    if not WIDE:
        return np.ones(k)
    levels = np.array([10, -10, 5, -5, 0])
    if k % 512:
        return np.exp2(np.random.permutation(np.resize(levels, k // 32))).repeat(32)
    a = np.empty((k // 512, 16))
    for p in range(k // 512):
        a[p, :8] = np.random.permutation(np.resize(levels, 8))
        for g in range(8):
            far = levels[np.abs(levels - a[p, g]) >= 10]
            a[p, g + 8] = far[np.random.randint(len(far))]
    return np.exp2(a.ravel()).repeat(32)


BF16 = ml_dtypes.bfloat16


def bf(x):
    return np.asarray(x, np.float32).astype(BF16)


def f64(x):
    return np.asarray(x).astype(np.float64)


E2M1 = np.array([0.0, 0.5, 1.0, 1.5, 2.0, 3.0, 4.0, 6.0, -0.0, -0.5, -1.0, -1.5, -2.0, -3.0, -4.0, -6.0])


def pack_weight(w, fmt):
    k, n = w.shape
    w = f64(bf(w)).reshape(k // 32, 32, n)
    amax = np.abs(w).max(1)
    if fmt == "e4m3":
        byte = np.frexp(amax)[1] - 1 + 127 - 7
    else:
        mant, ex = np.frexp(amax / 6.0)
        byte = np.where(mant > 0.5, ex, ex - 1) + 127
    byte = np.clip(np.where(amax > 0, byte, 1), 1, 254)
    scaled = (w * np.exp2(127.0 - byte)[:, None, :]).reshape(k, n).astype(np.float32)
    by_word = np.ascontiguousarray(scaled.reshape(k // 512, 128, 4, n).transpose(0, 1, 3, 2))
    if fmt == "e4m3":
        words = by_word.astype(ml_dtypes.float8_e4m3fn).view(np.uint8)
    else:
        c = by_word.astype(ml_dtypes.float4_e2m1fn).view(np.uint8) & 0xF
        words = c[..., 0::2] | (c[..., 1::2] << 4)
    return np.ascontiguousarray(words), np.ascontiguousarray(byte.astype(np.uint8).reshape(k // 512, 16, n))


def unpack_weight(words, scales, fmt):
    g, p, n, _ = words.shape
    if fmt == "e4m3":
        vals = np.ascontiguousarray(words).view(ml_dtypes.float8_e4m3fn).astype(np.float64)
    else:
        nib = np.empty((g, p, n, 4), np.uint8)
        nib[..., 0::2] = words & 0xF
        nib[..., 1::2] = words >> 4
        vals = E2M1[nib]
    vals = vals * np.repeat(np.exp2(scales.astype(np.float64) - 127.0), 8, axis=1)[..., None]
    return vals.transpose(0, 1, 3, 2).reshape(g * 512, n)

def planes(Y):
    n, m = Y.shape
    b = f64(bf(Y)).reshape(n // 32, 32, m)
    amax = np.abs(b).max(1)
    byte = np.clip(np.where(amax > 0, np.frexp(amax)[1] - 1 + 127 - 7, 1), 1, 254)
    codes = (b * np.exp2(127.0 - byte)[:, None, :]).reshape(n, m).astype(np.float32).astype(ml_dtypes.float8_e4m3fn).view(np.uint8)
    words = codes.reshape(n // 512, 128, 4, m).transpose(0, 1, 3, 2)
    return np.ascontiguousarray(words), np.ascontiguousarray(byte.astype(np.uint8).reshape(n // 512, 16, m))


N, D, Q, V, E = 512, 1024, 512, 2048, 1024


def vocab_distribution(z):
    w = np.exp(z - z.max(axis=-1, keepdims=True))
    return w / w.sum(axis=-1, keepdims=True)


def kseq_residual(p, q):
    m = np.minimum(q, p / 2.0)
    beta = np.sum(m, axis=-1)
    acc = 1.0 - np.square(1.0 - beta)
    return (p - m * acc[:, None] / beta[:, None]) / (1.0 - acc)[:, None]


def setup_inputs():
    s, u, t = mx_kscale(D), mx_kscale(Q), mx_kscale(V)
    hp = bf(np.random.standard_normal((N, D)) * s)
    wp_words, wp_scales = pack_weight(np.random.standard_normal((D, V)) / np.sqrt(D) / s[:, None], "e4m3")
    hq = bf(np.random.standard_normal((N, Q)) * u)
    wq_words, wq_scales = pack_weight(np.random.standard_normal((Q, V)) / np.sqrt(Q) / u[:, None], "e4m3")
    g = bf(np.random.standard_normal(V) * 0.35 * np.sqrt(V) * t)
    e_words, e_scales = pack_weight(np.random.standard_normal((V, E)) / t[:, None], "e4m3")
    return {"hp": hp,
            "wp_words": wp_words, "wp_scales": wp_scales,
            "hq": hq,
            "wq_words": wq_words, "wq_scales": wq_scales,
            "g": g,
            "e_words": e_words, "e_scales": e_scales}


def core(hp, wp_words, wp_scales, hq, wq_words, wq_scales, g, e_words, e_scales):
    p = vocab_distribution(mxq(f64(hp), 1, "e4m3") @ unpack_weight(wp_words, wp_scales, "e4m3"))
    q = vocab_distribution(mxq(f64(hq), 1, "e4m3") @ unpack_weight(wq_words, wq_scales, "e4m3"))
    r = kseq_residual(p, q)
    a = r * f64(g)[None, :]
    return mxq(a, 1, "e4m3") @ unpack_weight(e_words, e_scales, "e4m3")


def reference(hp, wp_words, wp_scales, hq, wq_words, wq_scales, g, e_words, e_scales):
    R_out = core(hp, wp_words, wp_scales, hq, wq_words, wq_scales, g, e_words, e_scales)
    words, scales = planes(R_out.T)
    return R_out, words, scales

@@ -1,0 +1,635 @@
+from contextlib import ExitStack
+
+import concourse.mybir as mybir
+from concourse.masks import make_identity
+
+N, D, Q, V, E = 512, 1024, 512, 2048, 1024
+
+FLOPS = 2 * N * V * (D + Q) + 2 * N * V * E
+
+F32 = mybir.dt.float32
+BF16 = mybir.dt.bfloat16
+I32 = mybir.dt.int32
+U32 = mybir.dt.uint32
+U8 = mybir.dt.uint8
+FP8X4 = mybir.dt.float8_e4m3fn_x4
+ALU = mybir.AluOpType
+ACT = mybir.ActivationFunctionType
+AX = mybir.AxisListType
+
+P = 128
+TILES = N // P
+BANK = 512
+VB = V // BANK
+
+
+def tile_spectrkseqresidualexpectedembedding_x2_kernel(
+    tc, hp, wp_words, wp_scales, hq, wq_words, wq_scales, g, e_words, e_scales, out, out_words, out_scales
+):
+    nc = tc.nc
+
+    with ExitStack() as ctx:
+        keep = ctx.enter_context(tc.tile_pool(name="keep", bufs=1))
+        hpool = ctx.enter_context(tc.tile_pool(name="hpool", bufs=2))
+        soft = ctx.enter_context(tc.tile_pool(name="soft", bufs=3))
+        work = ctx.enter_context(tc.tile_pool(name="work", bufs=2))
+        psum = ctx.enter_context(tc.psum_pool(name="psum", bufs=1))
+        ctx.enter_context(tc.manual_schedule())
+
+        turn = {"bank": 0}
+
+        def bank(b=None):
+            if b is None:
+                b = turn["bank"] % 8
+                turn["bank"] += 1
+            return psum.tile([P, BANK], F32, name="bank%d" % b, tag="bank%d" % b)
+
+        w_sc = keep.tile([P, V], U8, name="w_sc", align_bytes=256)
+        nc.vector.memset(w_sc[:].bitcast(I32), 0)
+        ident = keep.tile([P, P], F32, name="ident", align_bytes=64)
+        make_identity(nc, ident[:])
+        warm = keep.tile([P, 1], F32, name="warm")
+        nc.vector.memset(warm[:], 0.0)
+        warm_out = keep.tile([P, 1], F32, name="warm_out")
+        nc.scalar.activation(out=warm_out[:], in_=warm[:], func=ACT.Exp)
+
+        g_row = keep.tile([P, V], BF16, name="g_row", align_bytes=256)
+        nc.vector.memset(g_row[:].bitcast(I32), 0)
+        e_sc = keep.tile([P, E], U8, name="e_sc", align_bytes=256)
+        nc.vector.memset(e_sc[:].bitcast(I32), 0)
+        ones = keep.tile([P, P], BF16, name="ones", align_bytes=64)
+        nc.vector.memset(ones[:], 1.0)
+
+        xp = {}
+        xq = {}
+
+        def load_hp(i):
+            xp[i] = keep.tile([P, D], BF16, name="xp%d" % i, align_bytes=256)
+            nc.sync.dma_start(out=xp[i][:], in_=hp[P * i : P * (i + 1), :])
+
+        def load_hq(i):
+            xq[i] = keep.tile([P, Q], BF16, name="xq%d" % i, align_bytes=256)
+            nc.sync.dma_start(out=xq[i][:], in_=hq[P * i : P * (i + 1), :])
+
+        wp_t = {}
+        wq_t = {}
+        wp_flat = wp_words.rearrange("g p n t -> p g (n t)")
+        wq_flat = wq_words.rearrange("g p n t -> p g (n t)")
+        e_flat = e_words.rearrange("g p n t -> p g (n t)")
+
+        def load_wp(j):
+            wp_t[j] = keep.tile([P, 2, BANK], I32, name="wp%d" % j, align_bytes=256)
+            nc.sync.dma_start(out=wp_t[j][:], in_=wp_flat[:, :, 4 * BANK * j : 4 * BANK * (j + 1)].bitcast(I32))
+
+        def load_wq(j):
+            wq_t[j] = keep.tile([P, 1, BANK], I32, name="wq%d" % j, align_bytes=256)
+            nc.sync.dma_start(out=wq_t[j][:], in_=wq_flat[:, :, 4 * BANK * j : 4 * BANK * (j + 1)].bitcast(I32))
+
+        nc.gpsimd.dma_start(out=g_row[0:1, :], in_=g.rearrange("(o v) -> o v", o=1))
+        load_hq(0)
+        w_sc_words = w_sc[:].bitcast(I32)
+        for qd in range(4):
+            nc.sync.dma_start(
+                out=w_sc_words[32 * qd + 8 : 32 * qd + 12, :], in_=wq_scales.bitcast(I32)[0, 4 * qd : 4 * qd + 4, :]
+            )
+        for qd in range(4):
+            nc.sync.dma_start(
+                out=w_sc_words[32 * qd : 32 * qd + 8, :], in_=wp_scales.bitcast(I32)[:, 4 * qd : 4 * qd + 4, :]
+            )
+        load_wq(0)
+        load_hq(1)
+        for j in range(1, VB):
+            load_wq(j)
+        load_hp(0)
+        load_wp(0)
+        load_hp(1)
+        for j in range(1, VB):
+            load_wp(j)
+        for i in (2, 3):
+            load_hp(i)
+            load_hq(i)
+        e_sc_words = e_sc[:].bitcast(I32)
+        for qd in range(4):
+            nc.sync.dma_start(
+                out=e_sc_words[32 * qd : 32 * qd + 16, :], in_=e_scales.bitcast(I32)[:, 4 * qd : 4 * qd + 4, :]
+            )
+        e_t = {}
+        for k in range(4):
+            e_t[k] = keep.tile([P, E], I32, name="e%d" % k, align_bytes=256)
+            nc.sync.dma_start(out=e_t[k][:], in_=e_flat[:, k, :].bitcast(I32))
+
+        hpc, hps, hqc, hqs = {}, {}, {}, {}
+
+        gp, gq = {}, {}
+
+        def hp_turn(i, b=None):
+            t = bank(b)
+            words = xp[i][:].bitcast(F32)
+            for k in range(2):
+                for u in range(2):
+                    c = (2 * k + u) * P
+                    nc.tensor.transpose(t[:, c : c + P], words[:, 256 * k + u : 256 * (k + 1) : 2], ident[:])
+            gp[i] = hpool.tile([P, 4 * 256], BF16, name="gp", align_bytes=64)
+            nc.scalar.copy(
+                out=gp[i][:].bitcast(F32).rearrange("p (g r u) -> p g r u", g=2, u=2),
+                in_=t[:].rearrange("p (g u r) -> p g r u", g=2, u=2),
+            )
+
+        def hq_turn(i, b=None):
+            t = bank(b)
+            words = xq[i][:].bitcast(F32)
+            for u in range(2):
+                nc.tensor.transpose(t[:, u * P : (u + 1) * P], words[:, u:256:2], ident[:])
+            gq[i] = hpool.tile([P, 4 * 128], BF16, name="gq", align_bytes=64)
+            nc.scalar.copy(
+                out=gq[i][:].bitcast(F32).rearrange("p (r u) -> p r u", u=2),
+                in_=t[:, 0:256].rearrange("p (u r) -> p r u", u=2),
+            )
+
+        def hp_quant(i):
+            hpc[i] = keep.tile([P, 256], U32, name="hpc%d" % i, align_bytes=64)
+            hps[i] = keep.tile([P, 256], U8, name="hps%d" % i, align_bytes=64)
+            nc.vector.quantize_mx(out=hpc[i][:].bitcast(FP8X4), scales=hps[i][:], in_=gp[i][:])
+
+        def hq_quant(i):
+            hqc[i] = keep.tile([P, 128], U32, name="hqc%d" % i, align_bytes=64)
+            hqs[i] = keep.tile([P, 128], U8, name="hqs%d" % i, align_bytes=64)
+            nc.vector.quantize_mx(out=hqc[i][:].bitcast(FP8X4), scales=hqs[i][:], in_=gq[i][:])
+
+        st = {}
+
+        def open_tile(i):
+            s = {}
+            s["ep"] = soft.tile([P, V], F32, name="ep", align_bytes=64)
+            s["eq"] = soft.tile([P, V], F32, name="eq", align_bytes=64)
+            s["mx"] = keep.tile([P, 8], F32, name="mx%d" % i)
+            s["nm"] = keep.tile([P, 2], F32, name="nm%d" % i)
+            s["zs"] = keep.tile([P, 8], F32, name="zs%d" % i)
+            for n in ("zt", "rz"):
+                s[n] = keep.tile([P, 2], F32, name="%s%d" % (n, i))
+            for n in ("sc", "r4", "r2", "bt", "nd", "c", "rc", "al"):
+                s[n] = keep.tile([P, 1], F32, name="%s%d" % (n, i))
+            s["zp"], s["zq"] = {}, {}
+            st[i] = s
+
+        def mm_p(i, j, b=None):
+            z = bank(b)
+            for k in range(2):
+                nc.tensor.matmul_mx(
+                    out=z[:],
+                    lhsT=hpc[i][:, P * k : P * (k + 1)].bitcast(FP8X4),
+                    lhsT_scale=hps[i][:, P * k : P * (k + 1)],
+                    rhs=wp_t[j][:, k, :].bitcast(FP8X4),
+                    rhs_scale=w_sc[4 * k : P, BANK * j : BANK * (j + 1)],
+                    start=(k == 0),
+                    stop=(k == 1),
+                )
+            st[i]["zp"][j] = z
+
+        def mm_q(i, j, b=None):
+            z = bank(b)
+            nc.tensor.matmul_mx(
+                out=z[:],
+                lhsT=hqc[i][:].bitcast(FP8X4),
+                lhsT_scale=hqs[i][:],
+                rhs=wq_t[j][:, 0, :].bitcast(FP8X4),
+                rhs_scale=w_sc[8:P, BANK * j : BANK * (j + 1)],
+                start=True,
+                stop=True,
+            )
+            st[i]["zq"][j] = z
+
+        def vmax(i, which, j):
+            s = st[i]
+            c = 4 * which + j
+            z = s["zp" if which == 0 else "zq"][j]
+            nc.vector.tensor_reduce(out=s["mx"][:, c : c + 1], in_=z[:], axis=AX.X, op=ALU.max)
+
+        def vmax_all(i, which):
+            s = st[i]
+            nc.vector.tensor_reduce(
+                out=s["nm"][:, which : which + 1],
+                in_=s["mx"][:, 4 * which : 4 * which + 4],
+                axis=AX.X,
+                op=ALU.max,
+                negate=True,
+            )
+
+        def exps(i, which, j):
+            s = st[i]
+            z = s["zp" if which == 0 else "zq"][j]
+            dst = s["ep" if which == 0 else "eq"]
+            c = 4 * which + j
+            nc.scalar.activation(
+                out=dst[:, BANK * j : BANK * (j + 1)].rearrange("p (u q e) -> p u q e", u=2, e=2),
+                in_=z[:].rearrange("p (q u e) -> p u q e", u=2, e=2),
+                func=ACT.Exp,
+                bias=s["nm"][:, which : which + 1],
+                scale=1.0,
+                accum_out=s["zs"][:, c : c + 1],
+            )
+
+        def sums(i):
+            s = st[i]
+            nc.vector.tensor_reduce(
+                out=s["zt"][:], in_=s["zs"][:].rearrange("p (a j) -> p a j", a=2), axis=AX.X, op=ALU.add
+            )
+
+        def inv_sums(i):
+            s = st[i]
+            nc.vector.reciprocal(out=s["rz"][:], in_=s["zt"][:])
+            nc.gpsimd.tensor_scalar(
+                out=s["sc"][:], in0=s["zt"][:, 0:1], scalar1=2.0, scalar2=s["rz"][:, 1:2], op0=ALU.mult, op1=ALU.mult
+            )
+            nc.gpsimd.tensor_scalar(
+                out=s["r4"][:], in0=s["rz"][:, 0:1], scalar1=0.25, scalar2=0.0, op0=ALU.mult, op1=ALU.add
+            )
+            nc.gpsimd.tensor_scalar(
+                out=s["r2"][:], in0=s["rz"][:, 0:1], scalar1=-0.5, scalar2=0.0, op0=ALU.mult, op1=ALU.add
+            )
+
+        def vmin(i):
+            s = st[i]
+            s["m"] = work.tile([P, V], F32, name="m", align_bytes=64)
+            s["a"] = work.tile([P, V], BF16, name="a", align_bytes=64)
+            nc.vector.scalar_tensor_tensor(
+                out=s["m"][:],
+                in0=s["eq"][:],
+                scalar=s["sc"][:, 0:1],
+                in1=s["ep"][:],
+                op0=ALU.mult,
+                op1=ALU.min,
+                accum_out=s["bt"][:, 0:1],
+            )
+
+        def betas(i):
+            s = st[i]
+            nc.gpsimd.tensor_scalar(
+                out=s["c"][:], in0=s["bt"][:], scalar1=s["r2"][:, 0:1], scalar2=1.0, op0=ALU.mult, op1=ALU.add
+            )
+            nc.gpsimd.tensor_scalar(
+                out=s["nd"][:], in0=s["bt"][:], scalar1=s["r4"][:, 0:1], scalar2=-1.0, op0=ALU.mult, op1=ALU.add
+            )
+
+        def small_rc(i):
+            s = st[i]
+            nc.vector.reciprocal(out=s["rc"][:], in_=s["c"][:])
+
+        def small_al(i):
+            s = st[i]
+            nc.gpsimd.tensor_scalar(
+                out=s["al"][:],
+                in0=s["rc"][:],
+                scalar1=s["rc"][:, 0:1],
+                scalar2=s["rz"][:, 0:1],
+                op0=ALU.mult,
+                op1=ALU.mult,
+            )
+
+        def vsub(i, lo, hi):
+            s = st[i]
+            nc.vector.scalar_tensor_tensor(
+                out=s["m"][:, lo:hi],
+                in0=s["m"][:, lo:hi],
+                scalar=s["nd"][:, 0:1],
+                in1=s["ep"][:, lo:hi],
+                op0=ALU.mult,
+                op1=ALU.add,
+            )
+
+        def vgain(i, lo, hi):
+            s = st[i]
+            nc.vector.scalar_tensor_tensor(
+                out=s["a"][:, lo:hi],
+                in0=s["m"][:, lo:hi],
+                scalar=s["al"][:, 0:1],
+                in1=g_sb[:, lo:hi],
+                op0=ALU.mult,
+                op1=ALU.mult,
+            )
+
+        def diags(i):
+            s = st[i]
+            s["d1"] = work.tile([P, P], F32, name="d1", align_bytes=64)
+            s["d2"] = work.tile([P, P], F32, name="d2", align_bytes=64)
+            nc.gpsimd.tensor_scalar(
+                out=s["d1"][:], in0=ident[:], scalar1=s["al"][:, 0:1], scalar2=0.0, op0=ALU.mult, op1=ALU.add
+            )
+            nc.gpsimd.tensor_scalar(
+                out=s["d2"][:],
+                in0=ident[:],
+                scalar1=s["al"][:, 0:1],
+                scalar2=s["nd"][:, 0:1],
+                op0=ALU.mult,
+                op1=ALU.mult,
+            )
+
+        def mm_sub(i, k, b=None):
+            s = st[i]
+            t = bank(b)
+            s["r", k] = t
+            cols = slice(BANK * k, BANK * (k + 1))
+            nc.tensor.matmul(t[:], lhsT=s["d1"][:], rhs=s["ep"][:, cols], start=True, stop=False)
+            nc.tensor.matmul(t[:], lhsT=s["d2"][:], rhs=s["m"][:, cols], start=False, stop=True)
+
+        def vgain_t(i, k):
+            s = st[i]
+            cols = slice(BANK * k, BANK * (k + 1))
+            nc.vector.tensor_tensor(out=s["a"][:, cols], in0=s["r", k][:], in1=g_sb[:, cols], op=ALU.mult)
+
+        def open_a(i):
+            s = st[i]
+            s["ga"] = work.tile([P, 4 * BANK], BF16, name="ga", align_bytes=64)
+            s["ac"] = work.tile([P, BANK], U32, name="ac", align_bytes=64)
+            s["as"] = work.tile([P, BANK], U8, name="as_", align_bytes=64)
+
+        def a_turn(i, k0, nk, b=None):
+            s = st[i]
+            t = bank(b)
+            words = s["a"][:].bitcast(F32)
+            for k in range(nk):
+                for u in range(2):
+                    c = (2 * k + u) * P
+                    w = 256 * (k0 + k) + P * u
+                    nc.tensor.transpose(t[:, c : c + P], words[:, w : w + P], ident[:])
+            nc.scalar.copy(
+                out=s["ga"][:, BANK * k0 : BANK * (k0 + nk)].bitcast(F32).rearrange("p (g r u) -> p g r u", g=nk, u=2),
+                in_=t[:, 0 : 256 * nk].rearrange("p (g u r) -> p g r u", g=nk, u=2),
+            )
+
+        def a_quant(i, k0, nk):
+            s = st[i]
+            nc.vector.quantize_mx(
+                out=s["ac"][:, P * k0 : P * (k0 + nk)].bitcast(FP8X4),
+                scales=s["as"][:, P * k0 : P * (k0 + nk)],
+                in_=s["ga"][:, BANK * k0 : BANK * (k0 + nk)],
+            )
+
+        def open_out(i, b0=None, b1=None):
+            st[i]["o"] = [bank(b0), bank(b1)]
+
+        def mm_out(i, k, order=(0, 1, 2, 3)):
+            s = st[i]
+            for h in range(2):
+                nc.tensor.matmul_mx(
+                    out=s["o"][h][:],
+                    lhsT=s["ac"][:, P * k : P * (k + 1)].bitcast(FP8X4),
+                    lhsT_scale=s["as"][:, P * k : P * (k + 1)],
+                    rhs=e_t[k][:, BANK * h : BANK * (h + 1)].bitcast(FP8X4),
+                    rhs_scale=e_sc[4 * k : P, BANK * h : BANK * (h + 1)],
+                    start=(k == order[0]),
+                    stop=(k == order[3]),
+                )
+
+        ps = keep.tile([P, 2, N], U8, name="ps", align_bytes=256)
+
+        def open_evac(i):
+            s = st[i]
+            s["of"] = work.tile([P, E], F32, name="of", align_bytes=64)
+            s["ob"] = work.tile([P, E], BF16, name="ob", align_bytes=64)
+            s["pc"] = work.tile([P, 2, P], U32, name="pc", align_bytes=64)
+            s["go"] = work.tile([P, 2 * BANK], BF16, name="go", align_bytes=64)
+
+        def evac_b(i, h, copy):
+            s = st[i]
+            copy(
+                out=s["ob"][:, BANK * h : BANK * (h + 1)].rearrange("p (u q e) -> p u q e", u=2, e=2),
+                in_=s["o"][h][:].rearrange("p (q u e) -> p u q e", u=2, e=2),
+            )
+
+        def evac_f(i, h, copy):
+            s = st[i]
+            copy(out=s["of"][:, BANK * h : BANK * (h + 1)], in_=s["o"][h][:])
+
+        def store_f(i):
+            nc.sync.dma_start(out=out[P * i : P * (i + 1), :], in_=st[i]["of"][:])
+
+        def o_turn(i, k0, nk, copy, b=None):
+            s = st[i]
+            t = bank(b)
+            words = s["ob"][:].bitcast(F32)
+            for c in range(2 * nk):
+                w = 256 * k0 + P * c
+                nc.tensor.transpose(t[:, P * c : P * (c + 1)], words[:, w : w + P], ident[:])
+            copy(
+                out=s["go"][:, BANK * k0 : BANK * (k0 + nk)].bitcast(F32).rearrange("p (g r u) -> p g r u", g=nk, u=2),
+                in_=t[:, 0 : 256 * nk].rearrange("p (g u r) -> p g r u", g=nk, u=2),
+            )
+
+        def o_quant(i, k):
+            s = st[i]
+            nc.vector.quantize_mx(
+                out=s["pc"][:, k, :].bitcast(FP8X4),
+                scales=ps[:, k, P * i : P * (i + 1)],
+                in_=s["go"][:, BANK * k : BANK * (k + 1)],
+            )
+
+        pc_dram = out_words.rearrange("g p m t -> p g (m t)")
+
+        def store_codes(i):
+            nc.sync.dma_start(
+                out=pc_dram[:, :, 4 * P * i : 4 * P * (i + 1)].bitcast(I32),
+                in_=st[i]["pc"][:].bitcast(I32),
+            )
+
+        g_sb = keep.tile([P, V], BF16, name="g_sb", align_bytes=64)
+
+        open_tile(0)
+        open_tile(1)
+        hq_turn(0, 6)
+        hq_quant(0)
+        for j in range(VB):
+            mm_q(0, j, j)
+            vmax(0, 1, j)
+            if j == 0:
+                hq_turn(1, 7)
+                hq_quant(1)
+        vmax_all(0, 1)
+        for j in range(2):
+            mm_q(1, j, 4 + j)
+            vmax(1, 1, j)
+        hp_turn(0, 6)
+        hp_quant(0)
+        for j in range(2):
+            exps(0, 1, j)
+        hp_turn(1, 7)
+        mm_q(1, 2, 6)
+        vmax(1, 1, 2)
+        hp_quant(1)
+        mm_q(1, 3, 7)
+        vmax(1, 1, 3)
+        vmax_all(1, 1)
+        for j in range(2, VB):
+            exps(0, 1, j)
+        for j in range(VB):
+            mm_p(0, j, j)
+            vmax(0, 0, j)
+        vmax_all(0, 0)
+        for j in range(VB):
+            exps(1, 1, j)
+        for j in range(VB):
+            exps(0, 0, j)
+        for j in range(VB):
+            mm_p(1, j, 4 + j)
+            vmax(1, 0, j)
+        vmax_all(1, 0)
+        sums(0)
+        inv_sums(0)
+        for j in range(VB):
+            t = bank(j)
+            nc.tensor.matmul(t[:], lhsT=ones[:], rhs=g_row[:, BANK * j : BANK * (j + 1)], start=True, stop=True)
+            nc.scalar.copy(
+                out=g_sb[:, BANK * j : BANK * (j + 1)].rearrange("p (u q e) -> p u q e", u=2, e=2),
+                in_=t[:].rearrange("p (q u e) -> p u q e", u=2, e=2),
+            )
+        hp_turn(2)
+        hq_turn(2)
+        for j in range(VB):
+            exps(1, 0, j)
+
+        def start_out(i, b0=None, b1=None):
+            open_out(i, b0, b1)
+            for k in range(4):
+                mm_out(i, k)
+
+        def evacuate(i):
+            open_evac(i)
+            for h in range(2):
+                evac_b(i, h, nc.scalar.copy)
+            for h in range(2):
+                evac_f(i, h, nc.scalar.copy)
+            store_f(i)
+
+        for i in range(2):
+            n = i + 2
+            open_tile(n)
+            vmin(i)
+            betas(i)
+            if i == 0:
+                hp_quant(2)
+                hq_quant(2)
+            for j in range(VB):
+                mm_p(n, j)
+            if i == 1:
+                start_out(0)
+            for j in range(VB):
+                vmax(n, 0, j)
+                if j == 1:
+                    small_rc(i)
+                    small_al(i)
+                    diags(i)
+            vmax_all(n, 0)
+            sums(i + 1)
+            for j in range(VB):
+                exps(n, 0, j)
+            if i == 1:
+                evacuate(0)
+            mm_sub(i, 3)
+            vsub(i, 0, 1024)
+            vsub(i, 1024, 1536)
+            inv_sums(i + 1)
+            for j in range(VB):
+                mm_q(n, j)
+            if i == 1:
+                o_turn(0, 0, 2, nc.scalar.copy)
+            open_a(i)
+            vgain(i, 0, 1024)
+            a_turn(i, 0, 2)
+            vgain(i, 1024, 1536)
+            vgain_t(i, 3)
+            a_turn(i, 2, 2)
+            if i == 0:
+                hp_turn(3)
+                hq_turn(3)
+            for j in range(VB):
+                vmax(n, 1, j)
+            vmax_all(n, 1)
+            a_quant(i, 0, 4)
+            if i == 1:
+                o_quant(0, 0)
+                o_quant(0, 1)
+                store_codes(0)
+            else:
+                hp_quant(3)
+                hq_quant(3)
+            for j in range(VB):
+                exps(n, 1, j)
+
+        start_out(1, 5, 2)
+        vmin(2)
+        betas(2)
+        sums(3)
+        inv_sums(3)
+        small_rc(2)
+        small_al(2)
+        diags(2)
+        vmin(3)
+        betas(3)
+        evacuate(1)
+        mm_sub(2, 2, 3)
+        mm_sub(2, 3, 4)
+        o_turn(1, 0, 2, nc.scalar.copy, 6)
+        vsub(2, 0, 512)
+        vsub(2, 512, 1024)
+        small_rc(3)
+        small_al(3)
+        diags(3)
+        open_a(2)
+        open_a(3)
+        vgain(2, 0, 1024)
+        a_turn(2, 0, 2, 7)
+        vsub(3, 0, BANK)
+        mm_sub(3, 3, 0)
+        vgain_t(2, 2)
+        vgain_t(2, 3)
+        a_turn(2, 2, 2, 1)
+        vsub(3, BANK, 2 * BANK)
+        vgain(3, 0, BANK)
+        a_quant(2, 0, 4)
+        a_turn(3, 0, 1, 6)
+        start_out(2, 5, 2)
+        vsub(3, 2 * BANK, 3 * BANK)
+        vgain(3, BANK, 2 * BANK)
+        a_turn(3, 1, 1, 7)
+        open_evac(2)
+        evac_b(2, 0, nc.scalar.copy)
+        evac_b(2, 1, nc.scalar.copy)
+        vgain_t(3, 3)
+        a_turn(3, 3, 1, 3)
+        a_quant(3, 0, 2)
+        open_out(3, 4, 1)
+        mm_out(3, 0, (0, 1, 3, 2))
+        mm_out(3, 1, (0, 1, 3, 2))
+        vgain(3, 2 * BANK, 3 * BANK)
+        a_turn(3, 2, 1, 6)
+        o_turn(2, 0, 2, nc.scalar.copy, 7)
+        a_quant(3, 3, 1)
+        mm_out(3, 3, (0, 1, 3, 2))
+        o_quant(1, 0)
+        o_quant(1, 1)
+        store_codes(1)
+        a_quant(3, 2, 1)
+        mm_out(3, 2, (0, 1, 3, 2))
+        o_quant(2, 0)
+        o_quant(2, 1)
+        store_codes(2)
+        evac_f(2, 0, nc.scalar.copy)
+        open_evac(3)
+        evac_b(3, 0, nc.vector.tensor_copy)
+        evac_b(3, 1, nc.scalar.copy)
+        o_turn(3, 0, 1, nc.vector.tensor_copy, 0)
+        o_turn(3, 1, 1, nc.scalar.copy, 3)
+        o_quant(3, 0)
+        o_quant(3, 1)
+        evac_f(2, 1, nc.scalar.copy)
+        store_f(2)
+        evac_f(3, 0, nc.vector.tensor_copy)
+        evac_f(3, 1, nc.scalar.copy)
+        store_codes(3)
+        store_f(3)
+        ps_words = ps[:].rearrange("p g m -> p (g m)").bitcast(I32)
+        for qd in range(4):
+            nc.scalar.dma_start(
+                out=out_scales.bitcast(I32)[:, 4 * qd : 4 * qd + 4, :].rearrange("g r m -> r g m"),
+                in_=ps_words[32 * qd : 32 * qd + 4, :].rearrange("r (g m) -> r g m", g=2),
+            )

@@ -238,7 +238,10 @@ def tile_spectrkseqresidualexpectedembedding_x2_kernel(
         def inv_sums(i):
             s = st[i]
             nc.vector.reciprocal(out=s["rz"][:], in_=s["zt"][:])
-            nc.gpsimd.tensor_scalar(
+
+        def ratio(i):
+            s = st[i]
+            nc.vector.tensor_scalar(
                 out=s["sc"][:], in0=s["zt"][:, 0:1], scalar1=2.0, scalar2=s["rz"][:, 1:2], op0=ALU.mult, op1=ALU.mult
             )
             nc.gpsimd.tensor_scalar(
@@ -265,10 +268,10 @@ def tile_spectrkseqresidualexpectedembedding_x2_kernel(
         def betas(i):
             s = st[i]
             nc.gpsimd.tensor_scalar(
-                out=s["c"][:], in0=s["bt"][:], scalar1=s["r2"][:, 0:1], scalar2=1.0, op0=ALU.mult, op1=ALU.add
+                out=s["nd"][:], in0=s["bt"][:], scalar1=s["r4"][:, 0:1], scalar2=-1.0, op0=ALU.mult, op1=ALU.add
             )
             nc.gpsimd.tensor_scalar(
-                out=s["nd"][:], in0=s["bt"][:], scalar1=s["r4"][:, 0:1], scalar2=-1.0, op0=ALU.mult, op1=ALU.add
+                out=s["c"][:], in0=s["bt"][:], scalar1=s["r2"][:, 0:1], scalar2=1.0, op0=ALU.mult, op1=ALU.add
             )
 
         def small_rc(i):
@@ -473,19 +476,22 @@ def tile_spectrkseqresidualexpectedembedding_x2_kernel(
             mm_p(1, j, 4 + j)
             vmax(1, 0, j)
         vmax_all(1, 0)
-        sums(0)
-        inv_sums(0)
+        hp_turn(2, 0)
+        hq_turn(2, 1)
         for j in range(VB):
-            t = bank(j)
+            t = bank((2 + j) % 4)
             nc.tensor.matmul(t[:], lhsT=ones[:], rhs=g_row[:, BANK * j : BANK * (j + 1)], start=True, stop=True)
             nc.scalar.copy(
                 out=g_sb[:, BANK * j : BANK * (j + 1)].rearrange("p (u q e) -> p u q e", u=2, e=2),
                 in_=t[:].rearrange("p (q u e) -> p u q e", u=2, e=2),
             )
-        hp_turn(2)
-        hq_turn(2)
+        sums(0)
+        inv_sums(0)
+        ratio(0)
         for j in range(VB):
             exps(1, 0, j)
+        hp_quant(2)
+        hq_quant(2)
 
         def start_out(i, b0=None, b1=None):
             open_out(i, b0, b1)
@@ -505,12 +511,10 @@ def tile_spectrkseqresidualexpectedembedding_x2_kernel(
             open_tile(n)
             vmin(i)
             betas(i)
-            if i == 0:
-                hp_quant(2)
-                hq_quant(2)
             for j in range(VB):
                 mm_p(n, j)
             if i == 1:
+                a_quant(0, 0, 4)
                 start_out(0)
             for j in range(VB):
                 vmax(n, 0, j)
@@ -522,8 +526,6 @@ def tile_spectrkseqresidualexpectedembedding_x2_kernel(
             sums(i + 1)
             for j in range(VB):
                 exps(n, 0, j)
-            if i == 1:
-                evacuate(0)
             mm_sub(i, 3)
             vsub(i, 0, 1024)
             vsub(i, 1024, 1536)
@@ -531,101 +533,106 @@ def tile_spectrkseqresidualexpectedembedding_x2_kernel(
             for j in range(VB):
                 mm_q(n, j)
             if i == 1:
-                o_turn(0, 0, 2, nc.scalar.copy)
+                evacuate(0)
+            else:
+                hp_turn(3)
+                hq_turn(3)
             open_a(i)
             vgain(i, 0, 1024)
             a_turn(i, 0, 2)
-            vgain(i, 1024, 1536)
-            vgain_t(i, 3)
-            a_turn(i, 2, 2)
-            if i == 0:
-                hp_turn(3)
-                hq_turn(3)
+            ratio(i + 1)
             for j in range(VB):
                 vmax(n, 1, j)
             vmax_all(n, 1)
-            a_quant(i, 0, 4)
-            if i == 1:
-                o_quant(0, 0)
-                o_quant(0, 1)
-                store_codes(0)
-            else:
-                hp_quant(3)
-                hq_quant(3)
             for j in range(VB):
                 exps(n, 1, j)
+            vgain(i, 1024, 1536)
+            vgain_t(i, 3)
+            a_turn(i, 2, 2)
+            if i == 1:
+                o_turn(0, 0, 2, nc.scalar.copy)
+            if i == 0:
+                hp_quant(3)
+                hq_quant(3)
+            else:
+                a_quant(1, 0, 2)
 
-        start_out(1, 5, 2)
         vmin(2)
         betas(2)
+        a_quant(1, 2, 2)
+        start_out(1, 5, 2)
         sums(3)
+        o_quant(0, 0)
+        o_quant(0, 1)
+        store_codes(0)
         inv_sums(3)
         small_rc(2)
         small_al(2)
         diags(2)
+        ratio(3)
+        mm_sub(2, 3, 3)
+        vsub(2, 0, 512)
         vmin(3)
         betas(3)
         evacuate(1)
-        mm_sub(2, 2, 3)
-        mm_sub(2, 3, 4)
-        o_turn(1, 0, 2, nc.scalar.copy, 6)
-        vsub(2, 0, 512)
-        vsub(2, 512, 1024)
-        small_rc(3)
-        small_al(3)
-        diags(3)
+        vsub(2, 512, 1536)
         open_a(2)
         open_a(3)
         vgain(2, 0, 1024)
+        small_rc(3)
+        small_al(3)
+        diags(3)
         a_turn(2, 0, 2, 7)
-        vsub(3, 0, BANK)
         mm_sub(3, 3, 0)
-        vgain_t(2, 2)
+        vgain(2, 1024, 1536)
         vgain_t(2, 3)
         a_turn(2, 2, 2, 1)
-        vsub(3, BANK, 2 * BANK)
-        vgain(3, 0, BANK)
-        a_quant(2, 0, 4)
-        a_turn(3, 0, 1, 6)
-        start_out(2, 5, 2)
+        vsub(3, 0, 2 * BANK)
         vsub(3, 2 * BANK, 3 * BANK)
-        vgain(3, BANK, 2 * BANK)
-        a_turn(3, 1, 1, 7)
-        open_evac(2)
-        evac_b(2, 0, nc.scalar.copy)
-        evac_b(2, 1, nc.scalar.copy)
         vgain_t(3, 3)
         a_turn(3, 3, 1, 3)
-        a_quant(3, 0, 2)
-        open_out(3, 4, 1)
-        mm_out(3, 0, (0, 1, 3, 2))
-        mm_out(3, 1, (0, 1, 3, 2))
-        vgain(3, 2 * BANK, 3 * BANK)
-        a_turn(3, 2, 1, 6)
-        o_turn(2, 0, 2, nc.scalar.copy, 7)
+        vgain(3, 0, BANK)
+        a_turn(3, 0, 1, 4)
+        o_turn(1, 0, 2, nc.scalar.copy, 6)
+        a_quant(2, 0, 2)
+        a_quant(2, 2, 2)
+        start_out(2, 5, 2)
+        vgain(3, BANK, 2 * BANK)
+        a_turn(3, 1, 1, 1)
         a_quant(3, 3, 1)
-        mm_out(3, 3, (0, 1, 3, 2))
+        vgain(3, 2 * BANK, 3 * BANK)
+        a_turn(3, 2, 1, 7)
+        a_quant(3, 0, 1)
+        a_quant(3, 1, 1)
+        open_out(3, 0, 4)
+        mm_out(3, 3, (3, 0, 1, 2))
+        mm_out(3, 0, (3, 0, 1, 2))
+        mm_out(3, 1, (3, 0, 1, 2))
         o_quant(1, 0)
         o_quant(1, 1)
         store_codes(1)
+        open_evac(2)
+        evac_b(2, 0, nc.scalar.copy)
         a_quant(3, 2, 1)
-        mm_out(3, 2, (0, 1, 3, 2))
-        o_quant(2, 0)
-        o_quant(2, 1)
-        store_codes(2)
-        evac_f(2, 0, nc.scalar.copy)
+        mm_out(3, 2, (3, 0, 1, 2))
+        evac_b(2, 1, nc.scalar.copy)
+        o_turn(2, 0, 2, nc.scalar.copy, 6)
+        evac_f(2, 0, nc.vector.tensor_copy)
         open_evac(3)
         evac_b(3, 0, nc.vector.tensor_copy)
         evac_b(3, 1, nc.scalar.copy)
-        o_turn(3, 0, 1, nc.vector.tensor_copy, 0)
+        o_turn(3, 0, 1, nc.vector.tensor_copy, 1)
         o_turn(3, 1, 1, nc.scalar.copy, 3)
+        o_quant(2, 0)
+        o_quant(2, 1)
+        store_codes(2)
         o_quant(3, 0)
         o_quant(3, 1)
-        evac_f(2, 1, nc.scalar.copy)
-        store_f(2)
         evac_f(3, 0, nc.vector.tensor_copy)
+        evac_f(2, 1, nc.scalar.copy)
         evac_f(3, 1, nc.scalar.copy)
         store_codes(3)
+        store_f(2)
         store_f(3)
         ps_words = ps[:].rearrange("p g m -> p (g m)").bitcast(I32)
         for qd in range(4):

@@ -85,7 +85,6 @@ def tile_spectrkseqresidualexpectedembedding_x2_kernel(
             wq_t[j] = keep.tile([P, 1, BANK], I32, name="wq%d" % j, align_bytes=256)
             nc.sync.dma_start(out=wq_t[j][:], in_=wq_flat[:, :, 4 * BANK * j : 4 * BANK * (j + 1)].bitcast(I32))
 
-        nc.gpsimd.dma_start(out=g_row[0:1, :], in_=g.rearrange("(o v) -> o v", o=1))
         load_hq(0)
         w_sc_words = w_sc[:].bitcast(I32)
         for qd in range(4):
@@ -93,17 +92,18 @@ def tile_spectrkseqresidualexpectedembedding_x2_kernel(
                 out=w_sc_words[32 * qd + 8 : 32 * qd + 12, :], in_=wq_scales.bitcast(I32)[0, 4 * qd : 4 * qd + 4, :]
             )
         for qd in range(4):
-            nc.sync.dma_start(
+            nc.scalar.dma_start(
                 out=w_sc_words[32 * qd : 32 * qd + 8, :], in_=wp_scales.bitcast(I32)[:, 4 * qd : 4 * qd + 4, :]
             )
+        nc.scalar.dma_start(out=g_row[0:1, :], in_=g.rearrange("(o v) -> o v", o=1))
         load_wq(0)
+        load_wq(1)
         load_hq(1)
-        for j in range(1, VB):
-            load_wq(j)
+        load_wq(2)
         load_hp(0)
-        load_wp(0)
+        load_wq(3)
         load_hp(1)
-        for j in range(1, VB):
+        for j in range(VB):
             load_wp(j)
         for i in (2, 3):
             load_hp(i)
@@ -407,6 +407,10 @@ def tile_spectrkseqresidualexpectedembedding_x2_kernel(
         def store_f(i):
             nc.sync.dma_start(out=out[P * i : P * (i + 1), :], in_=st[i]["of"][:])
 
+        def store_f_half(i, h, queue):
+            cols = slice(BANK * h, BANK * (h + 1))
+            queue.dma_start(out=out[P * i : P * (i + 1), cols], in_=st[i]["of"][:, cols])
+
         def o_turn(i, k0, nk, copy, b=None):
             s = st[i]
             t = bank(b)
@@ -435,63 +439,88 @@ def tile_spectrkseqresidualexpectedembedding_x2_kernel(
                 in_=st[i]["pc"][:].bitcast(I32),
             )
 
+        def store_scales():
+            ps_words = ps[:].rearrange("p g m -> p (g m)").bitcast(I32)
+            for qd in range(4):
+                nc.sync.dma_start(
+                    out=out_scales.bitcast(I32)[:, 4 * qd : 4 * qd + 4, :].rearrange("g r m -> r g m"),
+                    in_=ps_words[32 * qd : 32 * qd + 4, :].rearrange("r (g m) -> r g m", g=2),
+                )
+
         g_sb = keep.tile([P, V], BF16, name="g_sb", align_bytes=64)
 
         open_tile(0)
         open_tile(1)
-        hq_turn(0, 6)
+        hq_turn(0, 4)
         hq_quant(0)
         for j in range(VB):
             mm_q(0, j, j)
             vmax(0, 1, j)
-            if j == 0:
-                hq_turn(1, 7)
+            if j == 1:
+                hq_turn(1, 5)
                 hq_quant(1)
-        vmax_all(0, 1)
-        for j in range(2):
-            mm_q(1, j, 4 + j)
-            vmax(1, 1, j)
-        hp_turn(0, 6)
-        hp_quant(0)
-        for j in range(2):
-            exps(0, 1, j)
+            if j == 2:
+                hp_turn(0, 6)
+                hp_quant(0)
         hp_turn(1, 7)
-        mm_q(1, 2, 6)
-        vmax(1, 1, 2)
-        hp_quant(1)
-        mm_q(1, 3, 7)
-        vmax(1, 1, 3)
-        vmax_all(1, 1)
-        for j in range(2, VB):
-            exps(0, 1, j)
+        vmax_all(0, 1)
         for j in range(VB):
-            mm_p(0, j, j)
-            vmax(0, 0, j)
+            exps(0, 1, j)
+        hp_quant(1)
+        mm_p(0, 0, 4)
+        mm_q(1, 0, 0)
+        mm_p(0, 1, 5)
+        mm_q(1, 1, 1)
+        mm_p(0, 2, 6)
+        mm_p(0, 3, 7)
+        mm_q(1, 2, 2)
+        mm_q(1, 3, 3)
+        vmax(0, 0, 0)
+        vmax(1, 1, 0)
+        vmax(0, 0, 1)
+        vmax(1, 1, 1)
+        vmax(0, 0, 2)
+        vmax(0, 0, 3)
+        vmax(1, 1, 2)
         vmax_all(0, 0)
         for j in range(VB):
-            exps(1, 1, j)
-        for j in range(VB):
             exps(0, 0, j)
+        vmax(1, 1, 3)
         for j in range(VB):
             mm_p(1, j, 4 + j)
-            vmax(1, 0, j)
-        vmax_all(1, 0)
+        vmax(1, 0, 0)
+        vmax_all(1, 1)
+        for j in range(2):
+            exps(1, 1, j)
         hp_turn(2, 0)
         hq_turn(2, 1)
+        for j in range(2, VB):
+            exps(1, 1, j)
+        vmax(1, 0, 1)
+        vmax(1, 0, 2)
+        sums(0)
+        vmax(1, 0, 3)
+        inv_sums(0)
+        vmax_all(1, 0)
+        ratio(0)
+        hp_quant(2)
+        vmin(0)
+        betas(0)
+        hq_quant(2)
+        open_tile(2)
         for j in range(VB):
-            t = bank((2 + j) % 4)
+            mm_p(2, j, (2, 3, 0, 1)[j])
+        vmax(2, 0, 0)
+        for j in range(VB):
+            exps(1, 0, j)
+        for j in range(VB):
+            t = bank(4 + j)
             nc.tensor.matmul(t[:], lhsT=ones[:], rhs=g_row[:, BANK * j : BANK * (j + 1)], start=True, stop=True)
             nc.scalar.copy(
                 out=g_sb[:, BANK * j : BANK * (j + 1)].rearrange("p (u q e) -> p u q e", u=2, e=2),
                 in_=t[:].rearrange("p (q u e) -> p u q e", u=2, e=2),
             )
-        sums(0)
-        inv_sums(0)
-        ratio(0)
-        for j in range(VB):
-            exps(1, 0, j)
-        hp_quant(2)
-        hq_quant(2)
+        turn["bank"] = 4
 
         def start_out(i, b0=None, b1=None):
             open_out(i, b0, b1)
@@ -506,29 +535,35 @@ def tile_spectrkseqresidualexpectedembedding_x2_kernel(
                 evac_f(i, h, nc.scalar.copy)
             store_f(i)
 
+        tensor_blocks = {0: (3,), 1: (3,)}
+        lo = {i: BANK * (VB - len(tensor_blocks[i])) for i in tensor_blocks}
+
         for i in range(2):
             n = i + 2
-            open_tile(n)
-            vmin(i)
-            betas(i)
-            for j in range(VB):
-                mm_p(n, j)
+            if i == 1:
+                open_tile(3)
+                vmin(1)
+                betas(1)
+                for j in range(VB):
+                    mm_p(3, j)
             if i == 1:
                 a_quant(0, 0, 4)
                 start_out(0)
             for j in range(VB):
-                vmax(n, 0, j)
+                if n == 3 or j > 0:
+                    vmax(n, 0, j)
                 if j == 1:
                     small_rc(i)
                     small_al(i)
                     diags(i)
+            vsub(i, 0, 512)
             vmax_all(n, 0)
             sums(i + 1)
             for j in range(VB):
                 exps(n, 0, j)
-            mm_sub(i, 3)
-            vsub(i, 0, 1024)
-            vsub(i, 1024, 1536)
+            for k in tensor_blocks[i]:
+                mm_sub(i, k)
+            vsub(i, 512, lo[i])
             inv_sums(i + 1)
             for j in range(VB):
                 mm_q(n, j)
@@ -543,10 +578,13 @@ def tile_spectrkseqresidualexpectedembedding_x2_kernel(
             ratio(i + 1)
             for j in range(VB):
                 vmax(n, 1, j)
+            if lo[i] > 1024:
+                vgain(i, 1024, lo[i])
+            else:
+                vgain_t(i, 2)
             vmax_all(n, 1)
             for j in range(VB):
                 exps(n, 1, j)
-            vgain(i, 1024, 1536)
             vgain_t(i, 3)
             a_turn(i, 2, 2)
             if i == 1:
@@ -560,7 +598,7 @@ def tile_spectrkseqresidualexpectedembedding_x2_kernel(
         vmin(2)
         betas(2)
         a_quant(1, 2, 2)
-        start_out(1, 5, 2)
+        start_out(1, 0, 3)
         sums(3)
         o_quant(0, 0)
         o_quant(0, 1)
@@ -570,73 +608,70 @@ def tile_spectrkseqresidualexpectedembedding_x2_kernel(
         small_al(2)
         diags(2)
         ratio(3)
-        mm_sub(2, 3, 3)
+        evacuate(1)
+        mm_sub(2, 3, 2)
+        mm_sub(2, 2, 4)
+        o_turn(1, 0, 2, nc.scalar.copy, 6)
         vsub(2, 0, 512)
         vmin(3)
         betas(3)
-        evacuate(1)
-        vsub(2, 512, 1536)
+        vsub(2, 512, 1024)
         open_a(2)
         open_a(3)
-        vgain(2, 0, 1024)
+        vgain(2, 0, 512)
         small_rc(3)
         small_al(3)
-        diags(3)
+        vgain(2, 512, 1024)
         a_turn(2, 0, 2, 7)
-        mm_sub(3, 3, 0)
-        vgain(2, 1024, 1536)
         vgain_t(2, 3)
-        a_turn(2, 2, 2, 1)
         vsub(3, 0, 2 * BANK)
-        vsub(3, 2 * BANK, 3 * BANK)
-        vgain_t(3, 3)
-        a_turn(3, 3, 1, 3)
+        vgain_t(2, 2)
+        a_turn(2, 2, 2, 1)
         vgain(3, 0, BANK)
         a_turn(3, 0, 1, 4)
-        o_turn(1, 0, 2, nc.scalar.copy, 6)
         a_quant(2, 0, 2)
+        vsub(3, 2 * BANK, 3 * BANK)
         a_quant(2, 2, 2)
-        start_out(2, 5, 2)
+        start_out(2, 0, 3)
         vgain(3, BANK, 2 * BANK)
-        a_turn(3, 1, 1, 1)
-        a_quant(3, 3, 1)
-        vgain(3, 2 * BANK, 3 * BANK)
-        a_turn(3, 2, 1, 7)
+        a_turn(3, 1, 1, 2)
+        vsub(3, 3 * BANK, 4 * BANK)
         a_quant(3, 0, 1)
+        vgain(3, 2 * BANK, 3 * BANK)
+        a_turn(3, 2, 1, 1)
+        open_evac(2)
+        evac_b(2, 0, nc.scalar.copy)
+        vgain(3, 3 * BANK, 4 * BANK)
+        a_turn(3, 3, 1, 7)
+        evac_b(2, 1, nc.scalar.copy)
+        open_out(3, 5, 4)
+        mm_out(3, 0)
         a_quant(3, 1, 1)
-        open_out(3, 0, 4)
-        mm_out(3, 3, (3, 0, 1, 2))
-        mm_out(3, 0, (3, 0, 1, 2))
-        mm_out(3, 1, (3, 0, 1, 2))
+        mm_out(3, 1)
+        a_quant(3, 2, 1)
+        mm_out(3, 2)
         o_quant(1, 0)
         o_quant(1, 1)
         store_codes(1)
-        open_evac(2)
-        evac_b(2, 0, nc.scalar.copy)
-        a_quant(3, 2, 1)
-        mm_out(3, 2, (3, 0, 1, 2))
-        evac_b(2, 1, nc.scalar.copy)
-        o_turn(2, 0, 2, nc.scalar.copy, 6)
         evac_f(2, 0, nc.vector.tensor_copy)
+        a_quant(3, 3, 1)
+        mm_out(3, 3)
+        evac_f(2, 1, nc.scalar.copy)
+        store_f(2)
         open_evac(3)
         evac_b(3, 0, nc.vector.tensor_copy)
         evac_b(3, 1, nc.scalar.copy)
+        o_turn(2, 0, 2, nc.scalar.copy, 6)
         o_turn(3, 0, 1, nc.vector.tensor_copy, 1)
-        o_turn(3, 1, 1, nc.scalar.copy, 3)
+        o_turn(3, 1, 1, nc.scalar.copy, 2)
         o_quant(2, 0)
         o_quant(2, 1)
         store_codes(2)
         o_quant(3, 0)
         o_quant(3, 1)
         evac_f(3, 0, nc.vector.tensor_copy)
-        evac_f(2, 1, nc.scalar.copy)
         evac_f(3, 1, nc.scalar.copy)
         store_codes(3)
-        store_f(2)
-        store_f(3)
-        ps_words = ps[:].rearrange("p g m -> p (g m)").bitcast(I32)
-        for qd in range(4):
-            nc.scalar.dma_start(
-                out=out_scales.bitcast(I32)[:, 4 * qd : 4 * qd + 4, :].rearrange("g r m -> r g m"),
-                in_=ps_words[32 * qd : 32 * qd + 4, :].rearrange("r (g m) -> r g m", g=2),
-            )
+        store_scales()
+        store_f_half(3, 0, nc.sync)
+        store_f_half(3, 1, nc.scalar)

@@ -31,7 +31,7 @@ def tile_spectrkseqresidualexpectedembedding_x2_kernel(
     with ExitStack() as ctx:
         keep = ctx.enter_context(tc.tile_pool(name="keep", bufs=1))
         hpool = ctx.enter_context(tc.tile_pool(name="hpool", bufs=2))
-        soft = ctx.enter_context(tc.tile_pool(name="soft", bufs=3))
+        soft = ctx.enter_context(tc.tile_pool(name="soft", bufs=4))
         work = ctx.enter_context(tc.tile_pool(name="work", bufs=2))
         psum = ctx.enter_context(tc.psum_pool(name="psum", bufs=1))
         ctx.enter_context(tc.manual_schedule())
@@ -44,6 +44,8 @@ def tile_spectrkseqresidualexpectedembedding_x2_kernel(
                 turn["bank"] += 1
             return psum.tile([P, BANK], F32, name="bank%d" % b, tag="bank%d" % b)
 
+        q_sc = keep.tile([P, V], U8, name="q_sc", align_bytes=256)
+        nc.vector.memset(q_sc[:].bitcast(I32), 0)
         w_sc = keep.tile([P, V], U8, name="w_sc", align_bytes=256)
         nc.vector.memset(w_sc[:].bitcast(I32), 0)
         ident = keep.tile([P, P], F32, name="ident", align_bytes=64)
@@ -86,28 +88,31 @@ def tile_spectrkseqresidualexpectedembedding_x2_kernel(
             nc.sync.dma_start(out=wq_t[j][:], in_=wq_flat[:, :, 4 * BANK * j : 4 * BANK * (j + 1)].bitcast(I32))
 
         load_hq(0)
+        load_wq(0)
         w_sc_words = w_sc[:].bitcast(I32)
         for qd in range(4):
             nc.sync.dma_start(
-                out=w_sc_words[32 * qd + 8 : 32 * qd + 12, :], in_=wq_scales.bitcast(I32)[0, 4 * qd : 4 * qd + 4, :]
+                out=q_sc[:].bitcast(I32)[32 * qd : 32 * qd + 4, :], in_=wq_scales.bitcast(I32)[0, 4 * qd : 4 * qd + 4, :]
             )
-        for qd in range(4):
-            nc.scalar.dma_start(
-                out=w_sc_words[32 * qd : 32 * qd + 8, :], in_=wp_scales.bitcast(I32)[:, 4 * qd : 4 * qd + 4, :]
-            )
-        nc.scalar.dma_start(out=g_row[0:1, :], in_=g.rearrange("(o v) -> o v", o=1))
-        load_wq(0)
         load_wq(1)
         load_hq(1)
         load_wq(2)
-        load_hp(0)
         load_wq(3)
+        load_hp(0)
+        for qd in range(4):
+            nc.sync.dma_start(
+                out=w_sc_words[32 * qd : 32 * qd + 8, :], in_=wp_scales.bitcast(I32)[:, 4 * qd : 4 * qd + 4, :]
+            )
+        load_wp(0)
+        load_hq(2)
+        load_wp(1)
         load_hp(1)
-        for j in range(VB):
-            load_wp(j)
+        load_wp(2)
+        load_wp(3)
+        nc.sync.dma_start(out=g_row[0:1, :], in_=g.rearrange("(o v) -> o v", o=1))
+        load_hq(3)
         for i in (2, 3):
             load_hp(i)
-            load_hq(i)
         e_sc_words = e_sc[:].bitcast(I32)
         for qd in range(4):
             nc.sync.dma_start(
@@ -193,7 +198,7 @@ def tile_spectrkseqresidualexpectedembedding_x2_kernel(
                 lhsT=hqc[i][:].bitcast(FP8X4),
                 lhsT_scale=hqs[i][:],
                 rhs=wq_t[j][:, 0, :].bitcast(FP8X4),
-                rhs_scale=w_sc[8:P, BANK * j : BANK * (j + 1)],
+                rhs_scale=q_sc[:, BANK * j : BANK * (j + 1)],
                 start=True,
                 stop=True,
             )
@@ -213,6 +218,28 @@ def tile_spectrkseqresidualexpectedembedding_x2_kernel(
                 axis=AX.X,
                 op=ALU.max,
                 negate=True,
+            )
+
+        def zcopy(i, which, j):
+            s = st[i]
+            if j == 0:
+                s["zb", which] = work.tile([P, V], BF16, name="zb", align_bytes=64)
+                s["zm", which] = work.tile([P, V // 2], BF16, name="zm", align_bytes=64)
+            z = s["zp" if which == 0 else "zq"][j]
+            nc.scalar.copy(out=s["zb", which][:, BANK * j : BANK * (j + 1)], in_=z[:])
+
+        def fold(i, which, step):
+            s = st[i]
+            zb, zm = s["zb", which], s["zm", which]
+            w = V >> (step + 1)
+            src, dst = (zb, zm) if step % 2 == 0 else (zm, zb)
+            nc.vector.tensor_tensor(out=dst[:, 0:w], in0=src[:, 0:w], in1=src[:, w : 2 * w], op=ALU.max)
+
+        def fold_end(i, which, step):
+            s = st[i]
+            src = s["zb", which] if step % 2 == 0 else s["zm", which]
+            nc.vector.tensor_reduce(
+                out=s["nm"][:, which : which + 1], in_=src[:, 0 : V >> step], axis=AX.X, op=ALU.max, negate=True
             )
 
         def exps(i, which, j):
@@ -238,17 +265,13 @@ def tile_spectrkseqresidualexpectedembedding_x2_kernel(
         def inv_sums(i):
             s = st[i]
             nc.vector.reciprocal(out=s["rz"][:], in_=s["zt"][:])
+            nc.scalar.activation(out=s["r4"][:], in_=s["rz"][:, 0:1], func=ACT.Copy, scale=0.25)
+            nc.scalar.activation(out=s["r2"][:], in_=s["rz"][:, 0:1], func=ACT.Copy, scale=-0.5)
 
         def ratio(i):
             s = st[i]
             nc.vector.tensor_scalar(
                 out=s["sc"][:], in0=s["zt"][:, 0:1], scalar1=2.0, scalar2=s["rz"][:, 1:2], op0=ALU.mult, op1=ALU.mult
-            )
-            nc.gpsimd.tensor_scalar(
-                out=s["r4"][:], in0=s["rz"][:, 0:1], scalar1=0.25, scalar2=0.0, op0=ALU.mult, op1=ALU.add
-            )
-            nc.gpsimd.tensor_scalar(
-                out=s["r2"][:], in0=s["rz"][:, 0:1], scalar1=-0.5, scalar2=0.0, op0=ALU.mult, op1=ALU.add
             )
 
         def vmin(i):
@@ -265,12 +288,15 @@ def tile_spectrkseqresidualexpectedembedding_x2_kernel(
                 accum_out=s["bt"][:, 0:1],
             )
 
-        def betas(i):
+        def small_nd(i):
             s = st[i]
-            nc.gpsimd.tensor_scalar(
+            nc.vector.tensor_scalar(
                 out=s["nd"][:], in0=s["bt"][:], scalar1=s["r4"][:, 0:1], scalar2=-1.0, op0=ALU.mult, op1=ALU.add
             )
-            nc.gpsimd.tensor_scalar(
+
+        def small_c(i):
+            s = st[i]
+            nc.vector.tensor_scalar(
                 out=s["c"][:], in0=s["bt"][:], scalar1=s["r2"][:, 0:1], scalar2=1.0, op0=ALU.mult, op1=ALU.add
             )
 
@@ -280,7 +306,7 @@ def tile_spectrkseqresidualexpectedembedding_x2_kernel(
 
         def small_al(i):
             s = st[i]
-            nc.gpsimd.tensor_scalar(
+            nc.vector.tensor_scalar(
                 out=s["al"][:],
                 in0=s["rc"][:],
                 scalar1=s["rc"][:, 0:1],
@@ -315,17 +341,8 @@ def tile_spectrkseqresidualexpectedembedding_x2_kernel(
             s = st[i]
             s["d1"] = work.tile([P, P], F32, name="d1", align_bytes=64)
             s["d2"] = work.tile([P, P], F32, name="d2", align_bytes=64)
-            nc.gpsimd.tensor_scalar(
-                out=s["d1"][:], in0=ident[:], scalar1=s["al"][:, 0:1], scalar2=0.0, op0=ALU.mult, op1=ALU.add
-            )
-            nc.gpsimd.tensor_scalar(
-                out=s["d2"][:],
-                in0=ident[:],
-                scalar1=s["al"][:, 0:1],
-                scalar2=s["nd"][:, 0:1],
-                op0=ALU.mult,
-                op1=ALU.mult,
-            )
+            nc.scalar.activation(out=s["d1"][:], in_=ident[:], func=ACT.Copy, scale=s["al"][:, 0:1])
+            nc.scalar.activation(out=s["d2"][:], in_=s["d1"][:], func=ACT.Copy, scale=s["nd"][:, 0:1])
 
         def mm_sub(i, k, b=None):
             s = st[i]
@@ -449,229 +466,287 @@ def tile_spectrkseqresidualexpectedembedding_x2_kernel(
 
         g_sb = keep.tile([P, V], BF16, name="g_sb", align_bytes=64)
 
-        open_tile(0)
-        open_tile(1)
-        hq_turn(0, 4)
-        hq_quant(0)
-        for j in range(VB):
-            mm_q(0, j, j)
-            vmax(0, 1, j)
-            if j == 1:
-                hq_turn(1, 5)
-                hq_quant(1)
-            if j == 2:
-                hp_turn(0, 6)
-                hp_quant(0)
-        hp_turn(1, 7)
-        vmax_all(0, 1)
-        for j in range(VB):
-            exps(0, 1, j)
-        hp_quant(1)
-        mm_p(0, 0, 4)
-        mm_q(1, 0, 0)
-        mm_p(0, 1, 5)
-        mm_q(1, 1, 1)
-        mm_p(0, 2, 6)
-        mm_p(0, 3, 7)
-        mm_q(1, 2, 2)
-        mm_q(1, 3, 3)
-        vmax(0, 0, 0)
-        vmax(1, 1, 0)
-        vmax(0, 0, 1)
-        vmax(1, 1, 1)
-        vmax(0, 0, 2)
-        vmax(0, 0, 3)
-        vmax(1, 1, 2)
-        vmax_all(0, 0)
-        for j in range(VB):
-            exps(0, 0, j)
-        vmax(1, 1, 3)
-        for j in range(VB):
-            mm_p(1, j, 4 + j)
-        vmax(1, 0, 0)
-        vmax_all(1, 1)
-        for j in range(2):
-            exps(1, 1, j)
-        hp_turn(2, 0)
-        hq_turn(2, 1)
-        for j in range(2, VB):
-            exps(1, 1, j)
-        vmax(1, 0, 1)
-        vmax(1, 0, 2)
-        sums(0)
-        vmax(1, 0, 3)
-        inv_sums(0)
-        vmax_all(1, 0)
-        ratio(0)
-        hp_quant(2)
-        vmin(0)
-        betas(0)
-        hq_quant(2)
-        open_tile(2)
-        for j in range(VB):
-            mm_p(2, j, (2, 3, 0, 1)[j])
-        vmax(2, 0, 0)
-        for j in range(VB):
-            exps(1, 0, j)
-        for j in range(VB):
-            t = bank(4 + j)
+        def g_turn(j, b=None):
+            t = bank(b)
             nc.tensor.matmul(t[:], lhsT=ones[:], rhs=g_row[:, BANK * j : BANK * (j + 1)], start=True, stop=True)
             nc.scalar.copy(
                 out=g_sb[:, BANK * j : BANK * (j + 1)].rearrange("p (u q e) -> p u q e", u=2, e=2),
                 in_=t[:].rearrange("p (q u e) -> p u q e", u=2, e=2),
             )
-        turn["bank"] = 4
 
-        def start_out(i, b0=None, b1=None):
-            open_out(i, b0, b1)
-            for k in range(4):
-                mm_out(i, k)
-
-        def evacuate(i):
-            open_evac(i)
-            for h in range(2):
-                evac_b(i, h, nc.scalar.copy)
-            for h in range(2):
-                evac_f(i, h, nc.scalar.copy)
-            store_f(i)
-
-        tensor_blocks = {0: (3,), 1: (3,)}
-        lo = {i: BANK * (VB - len(tensor_blocks[i])) for i in tensor_blocks}
-
-        for i in range(2):
-            n = i + 2
-            if i == 1:
-                open_tile(3)
-                vmin(1)
-                betas(1)
-                for j in range(VB):
-                    mm_p(3, j)
-            if i == 1:
-                a_quant(0, 0, 4)
-                start_out(0)
-            for j in range(VB):
-                if n == 3 or j > 0:
-                    vmax(n, 0, j)
-                if j == 1:
-                    small_rc(i)
-                    small_al(i)
-                    diags(i)
-            vsub(i, 0, 512)
-            vmax_all(n, 0)
-            sums(i + 1)
-            for j in range(VB):
-                exps(n, 0, j)
-            for k in tensor_blocks[i]:
-                mm_sub(i, k)
-            vsub(i, 512, lo[i])
-            inv_sums(i + 1)
-            for j in range(VB):
-                mm_q(n, j)
-            if i == 1:
-                evacuate(0)
-            else:
-                hp_turn(3)
-                hq_turn(3)
-            open_a(i)
-            vgain(i, 0, 1024)
-            a_turn(i, 0, 2)
-            ratio(i + 1)
-            for j in range(VB):
-                vmax(n, 1, j)
-            if lo[i] > 1024:
-                vgain(i, 1024, lo[i])
-            else:
-                vgain_t(i, 2)
-            vmax_all(n, 1)
-            for j in range(VB):
-                exps(n, 1, j)
-            vgain_t(i, 3)
-            a_turn(i, 2, 2)
-            if i == 1:
-                o_turn(0, 0, 2, nc.scalar.copy)
-            if i == 0:
-                hp_quant(3)
-                hq_quant(3)
-            else:
-                a_quant(1, 0, 2)
-
+        hq_turn(0, 0)
+        hq_quant(0)
+        open_tile(0)
+        mm_q(0, 1, 1)
+        hq_turn(1, 2)
+        mm_q(0, 2, 3)
+        mm_q(0, 0, 4)
+        hp_turn(0, 5)
+        mm_q(0, 3, 6)
+        hq_quant(1)
+        open_tile(1)
+        mm_q(1, 3, 7)
+        vmax(0, 1, 0)
+        vmax(0, 1, 1)
+        vmax(0, 1, 3)
+        vmax(0, 1, 2)
+        hq_turn(2, 0)
+        vmax_all(0, 1)
+        hp_quant(0)
+        mm_q(1, 2, 2)
+        mm_p(0, 0, 5)
+        mm_q(1, 0, 0)
+        vmax(1, 1, 3)
+        exps(0, 1, 2)
+        exps(0, 1, 3)
+        vmax(1, 1, 2)
+        hp_turn(1, 3)
+        exps(0, 1, 0)
+        vmax(1, 1, 0)
+        exps(0, 1, 1)
+        mm_p(0, 1, 6)
+        vmax(0, 0, 0)
+        hq_quant(2)
+        mm_p(0, 2, 3)
+        mm_p(0, 3, 4)
+        vmax(0, 0, 1)
+        g_turn(0, 1)
+        vmax(0, 0, 2)
+        vmax(0, 0, 3)
+        vmax_all(0, 0)
+        exps(0, 0, 3)
+        mm_q(1, 1, 1)
+        hp_quant(1)
+        exps(0, 0, 0)
+        vmax(1, 1, 1)
+        vmax_all(1, 1)
+        mm_p(1, 0, 4)
+        vmax(1, 0, 0)
+        exps(0, 0, 2)
+        mm_p(1, 2, 5)
+        vmax(1, 0, 2)
+        exps(0, 0, 1)
+        sums(0)
+        mm_p(1, 1, 3)
+        mm_p(1, 3, 6)
+        exps(1, 1, 3)
+        vmax(1, 0, 1)
+        exps(1, 1, 1)
+        hp_turn(2, 7)
+        inv_sums(0)
+        vmax(1, 0, 3)
+        ratio(0)
+        vmax_all(1, 0)
+        open_tile(2)
+        mm_q(2, 2, 1)
+        vmin(0)
+        mm_q(2, 1, 7)
+        hp_quant(2)
+        small_c(0)
+        exps(1, 0, 1)
+        exps(1, 1, 2)
+        small_nd(0)
+        hp_turn(3, 3)
+        mm_p(2, 3, 2)
+        exps(1, 1, 0)
+        mm_q(2, 0, 3)
+        exps(1, 0, 0)
+        vmax(2, 1, 1)
+        mm_p(2, 1, 0)
+        exps(1, 0, 3)
+        vmax(2, 1, 2)
+        exps(1, 0, 2)
+        vsub(0, 512, 1536)
+        vmax(2, 1, 0)
+        sums(1)
+        mm_p(2, 0, 4)
+        hp_quant(3)
+        small_rc(0)
+        inv_sums(1)
+        vmax(2, 0, 1)
+        ratio(1)
+        hq_turn(3, 6)
+        mm_p(2, 2, 5)
+        small_al(0)
+        vmax(2, 0, 2)
+        g_turn(2, 6)
+        vmax(2, 0, 0)
+        g_turn(3, 6)
+        vmax(2, 0, 3)
+        vsub(0, 0, 512)
+        vmax_all(2, 0)
+        vmin(1)
+        mm_q(2, 3, 6)
+        exps(2, 0, 3)
+        g_turn(1, 2)
+        exps(2, 0, 0)
+        exps(2, 0, 2)
+        vgain(0, 1024, 1536)
+        small_nd(1)
+        diags(0)
+        vmax(2, 1, 3)
+        vsub(1, 0, 512)
+        vmax_all(2, 1)
+        exps(2, 1, 3)
+        open_tile(3)
+        mm_p(3, 0, 2)
+        mm_sub(0, 3, 4)
+        exps(2, 1, 2)
+        exps(2, 1, 1)
+        vgain(0, 0, 1024)
+        exps(2, 0, 1)
+        small_c(1)
+        vmax(3, 0, 0)
+        vsub(1, 512, 1536)
+        small_rc(1)
+        vgain_t(0, 3)
+        hq_quant(3)
+        mm_p(3, 1, 5)
+        mm_p(3, 2, 6)
+        vmax(3, 0, 1)
+        mm_p(3, 3, 1)
+        exps(2, 1, 0)
+        vmax(3, 0, 3)
+        mm_q(3, 3, 7)
+        vmax(3, 0, 2)
+        open_a(0)
+        a_turn(0, 0, 2, 0)
+        a_turn(0, 2, 2, 3)
+        sums(2)
+        mm_q(3, 1, 4)
+        vmax(3, 1, 3)
+        vmax_all(3, 0)
+        small_al(1)
+        inv_sums(2)
+        a_quant(0, 0, 4)
+        mm_q(3, 2, 0)
+        ratio(2)
+        vmax(3, 1, 2)
+        exps(3, 0, 2)
+        mm_q(3, 0, 3)
+        vmax(3, 1, 1)
+        exps(3, 0, 1)
+        vmax(3, 1, 0)
+        diags(1)
+        vgain(1, 0, 1024)
+        mm_sub(1, 3, 6)
+        exps(3, 0, 3)
+        vmax_all(3, 1)
+        exps(3, 0, 0)
+        exps(3, 1, 1)
         vmin(2)
-        betas(2)
-        a_quant(1, 2, 2)
-        start_out(1, 0, 3)
+        vgain_t(1, 3)
+        open_out(0, 5, 1)
+        mm_out(0, 0)
+        exps(3, 1, 3)
+        exps(3, 1, 0)
+        vgain(1, 1024, 1536)
+        open_a(1)
+        a_turn(1, 0, 2, 2)
+        mm_out(0, 1)
+        mm_out(0, 2)
+        small_nd(2)
+        mm_out(0, 3)
+        exps(3, 1, 2)
+        a_turn(1, 2, 2, 4)
+        a_quant(1, 0, 2)
+        small_c(2)
         sums(3)
-        o_quant(0, 0)
-        o_quant(0, 1)
-        store_codes(0)
-        inv_sums(3)
-        small_rc(2)
-        small_al(2)
-        diags(2)
-        ratio(3)
-        evacuate(1)
-        mm_sub(2, 3, 2)
-        mm_sub(2, 2, 4)
-        o_turn(1, 0, 2, nc.scalar.copy, 6)
+        open_evac(0)
+        evac_f(0, 0, nc.scalar.copy)
+        open_out(1, 7, 3)
+        mm_out(1, 0)
         vsub(2, 0, 512)
-        vmin(3)
-        betas(3)
+        small_rc(2)
+        mm_out(1, 1)
+        inv_sums(3)
         vsub(2, 512, 1024)
-        open_a(2)
-        open_a(3)
+        ratio(3)
+        a_quant(1, 2, 2)
+        mm_out(1, 2)
+        small_al(2)
+        vmin(3)
+        diags(2)
         vgain(2, 0, 512)
-        small_rc(3)
-        small_al(3)
         vgain(2, 512, 1024)
-        a_turn(2, 0, 2, 7)
-        vgain_t(2, 3)
-        vsub(3, 0, 2 * BANK)
+        mm_sub(2, 2, 2)
+        small_nd(3)
+        small_c(3)
         vgain_t(2, 2)
-        a_turn(2, 2, 2, 1)
-        vgain(3, 0, BANK)
-        a_turn(3, 0, 1, 4)
+        evac_b(0, 1, nc.scalar.copy)
+        evac_f(0, 1, nc.scalar.copy)
+        mm_out(1, 3)
+        open_evac(1)
+        evac_f(1, 0, nc.scalar.copy)
+        open_a(2)
+        a_turn(2, 0, 2, 6)
+        vsub(3, 0, 1024)
+        mm_sub(2, 3, 0)
+        evac_b(0, 0, nc.scalar.copy)
+        small_rc(3)
         a_quant(2, 0, 2)
-        vsub(3, 2 * BANK, 3 * BANK)
+        evac_f(1, 1, nc.scalar.copy)
+        evac_b(1, 0, nc.scalar.copy)
+        small_al(3)
+        evac_b(1, 1, nc.scalar.copy)
+        o_turn(0, 0, 2, nc.scalar.copy, 4)
+        vsub(3, 1024, 1536)
+        vgain_t(2, 3)
+        open_out(2, 1, 2)
+        mm_out(2, 0)
+        vgain(3, 1024, 1536)
+        a_turn(2, 2, 2, 6)
+        o_turn(1, 0, 2, nc.scalar.copy, 5)
+        mm_out(2, 1)
+        vgain(3, 512, 1024)
+        vgain(3, 0, 512)
+        open_a(3)
+        a_turn(3, 1, 1, 7)
+        store_f(0)
         a_quant(2, 2, 2)
-        start_out(2, 0, 3)
-        vgain(3, BANK, 2 * BANK)
-        a_turn(3, 1, 1, 2)
-        vsub(3, 3 * BANK, 4 * BANK)
-        a_quant(3, 0, 1)
-        vgain(3, 2 * BANK, 3 * BANK)
-        a_turn(3, 2, 1, 1)
-        open_evac(2)
-        evac_b(2, 0, nc.scalar.copy)
-        vgain(3, 3 * BANK, 4 * BANK)
-        a_turn(3, 3, 1, 7)
-        evac_b(2, 1, nc.scalar.copy)
-        open_out(3, 5, 4)
-        mm_out(3, 0)
-        a_quant(3, 1, 1)
-        mm_out(3, 1)
-        a_quant(3, 2, 1)
-        mm_out(3, 2)
-        o_quant(1, 0)
+        a_turn(3, 2, 1, 3)
         o_quant(1, 1)
-        store_codes(1)
-        evac_f(2, 0, nc.vector.tensor_copy)
-        a_quant(3, 3, 1)
-        mm_out(3, 3)
+        a_turn(3, 0, 1, 0)
+        store_f(1)
+        vsub(3, 1536, 2048)
+        a_quant(3, 1, 1)
+        mm_out(2, 2)
+        a_quant(3, 0, 1)
+        mm_out(2, 3)
+        vgain(3, 1536, 2048)
+        o_quant(0, 0)
+        open_out(3, 4, 6)
+        mm_out(3, 0)
+        open_evac(2)
+        evac_b(2, 1, nc.scalar.copy)
+        o_quant(0, 1)
+        a_turn(3, 3, 1, 5)
         evac_f(2, 1, nc.scalar.copy)
-        store_f(2)
+        a_quant(3, 2, 1)
+        evac_b(2, 0, nc.scalar.copy)
+        o_quant(1, 0)
+        a_quant(3, 3, 1)
+        evac_f(2, 0, nc.vector.tensor_copy)
+        store_codes(0)
+        mm_out(3, 1)
+        mm_out(3, 2)
+        mm_out(3, 3)
         open_evac(3)
-        evac_b(3, 0, nc.vector.tensor_copy)
         evac_b(3, 1, nc.scalar.copy)
-        o_turn(2, 0, 2, nc.scalar.copy, 6)
-        o_turn(3, 0, 1, nc.vector.tensor_copy, 1)
-        o_turn(3, 1, 1, nc.scalar.copy, 2)
-        o_quant(2, 0)
-        o_quant(2, 1)
-        store_codes(2)
-        o_quant(3, 0)
-        o_quant(3, 1)
+        store_codes(1)
+        evac_b(3, 0, nc.vector.tensor_copy)
+        o_turn(2, 0, 2, nc.scalar.copy, 7)
         evac_f(3, 0, nc.vector.tensor_copy)
+        o_turn(3, 0, 1, nc.vector.tensor_copy, 3)
+        o_quant(2, 1)
+        store_f(2)
+        o_quant(2, 0)
+        o_turn(3, 1, 1, nc.scalar.copy, 0)
         evac_f(3, 1, nc.scalar.copy)
-        store_codes(3)
-        store_scales()
+        o_quant(3, 0)
         store_f_half(3, 0, nc.sync)
+        store_codes(2)
+        o_quant(3, 1)
         store_f_half(3, 1, nc.scalar)
+        store_scales()
+        store_codes(3)

@@ -18,9 +18,23 @@ ACT = mybir.ActivationFunctionType
 AX = mybir.AxisListType
 
 P = 128
-TILES = N // P
+K_PASS = 512
 BANK = 512
-VB = V // BANK
+BLOCKS = V // BANK
+QUADRANTS = 4
+P_SIDE, Q_SIDE = 0, 1
+
+
+def upe(bank):
+    return bank.rearrange("p (q u e) -> p u q e", u=2, e=2)
+
+
+def interleaved(turned, groups):
+    return turned.rearrange("p (g u r) -> p g r u", g=groups, u=2)
+
+
+def as_words(rows, groups):
+    return rows.bitcast(F32).rearrange("p (g r u) -> p g r u", g=groups, u=2)
 
 
 def tile_spectrkseqresidualexpectedembedding_x2_kernel(
@@ -30,40 +44,35 @@ def tile_spectrkseqresidualexpectedembedding_x2_kernel(
 
     with ExitStack() as ctx:
         keep = ctx.enter_context(tc.tile_pool(name="keep", bufs=1))
-        hpool = ctx.enter_context(tc.tile_pool(name="hpool", bufs=2))
         soft = ctx.enter_context(tc.tile_pool(name="soft", bufs=4))
         work = ctx.enter_context(tc.tile_pool(name="work", bufs=2))
         psum = ctx.enter_context(tc.psum_pool(name="psum", bufs=1))
         ctx.enter_context(tc.manual_schedule())
 
-        turn = {"bank": 0}
+        banks = {"free": list(range(8))}
 
-        def bank(b=None):
-            if b is None:
-                b = turn["bank"] % 8
-                turn["bank"] += 1
-            return psum.tile([P, BANK], F32, name="bank%d" % b, tag="bank%d" % b)
+        def take():
+            b = banks["free"][0]
+            banks["free"] = banks["free"][1:]
+            return psum.tile([P, BANK], F32, name="bank%d" % b, tag="bank%d" % b), b
+
+        def give(b):
+            banks["free"] = banks["free"] + [b]
 
         q_sc = keep.tile([P, V], U8, name="q_sc", align_bytes=256)
         nc.vector.memset(q_sc[:].bitcast(I32), 0)
-        w_sc = keep.tile([P, V], U8, name="w_sc", align_bytes=256)
-        nc.vector.memset(w_sc[:].bitcast(I32), 0)
-        ident = keep.tile([P, P], F32, name="ident", align_bytes=64)
-        make_identity(nc, ident[:])
-        warm = keep.tile([P, 1], F32, name="warm")
-        nc.vector.memset(warm[:], 0.0)
-        warm_out = keep.tile([P, 1], F32, name="warm_out")
-        nc.scalar.activation(out=warm_out[:], in_=warm[:], func=ACT.Exp)
-
+        p_sc = keep.tile([P, V], U8, name="p_sc", align_bytes=256)
+        nc.vector.memset(p_sc[:].bitcast(I32), 0)
         g_row = keep.tile([P, V], BF16, name="g_row", align_bytes=256)
         nc.vector.memset(g_row[:].bitcast(I32), 0)
         e_sc = keep.tile([P, E], U8, name="e_sc", align_bytes=256)
         nc.vector.memset(e_sc[:].bitcast(I32), 0)
+        ident = keep.tile([P, P], F32, name="ident", align_bytes=64)
+        make_identity(nc, ident[:])
         ones = keep.tile([P, P], BF16, name="ones", align_bytes=64)
-        nc.vector.memset(ones[:], 1.0)
+        nc.scalar.activation(out=ones[:], in_=ident[:], func=ACT.Exp, scale=0.0)
 
-        xp = {}
-        xq = {}
+        xp, xq, wp_t, wq_t, e_t = {}, {}, {}, {}, {}
 
         def load_hp(i):
             xp[i] = keep.tile([P, D], BF16, name="xp%d" % i, align_bytes=256)
@@ -73,8 +82,6 @@ def tile_spectrkseqresidualexpectedembedding_x2_kernel(
             xq[i] = keep.tile([P, Q], BF16, name="xq%d" % i, align_bytes=256)
             nc.sync.dma_start(out=xq[i][:], in_=hq[P * i : P * (i + 1), :])
 
-        wp_t = {}
-        wq_t = {}
         wp_flat = wp_words.rearrange("g p n t -> p g (n t)")
         wq_flat = wq_words.rearrange("g p n t -> p g (n t)")
         e_flat = e_words.rearrange("g p n t -> p g (n t)")
@@ -87,112 +94,114 @@ def tile_spectrkseqresidualexpectedembedding_x2_kernel(
             wq_t[j] = keep.tile([P, 1, BANK], I32, name="wq%d" % j, align_bytes=256)
             nc.sync.dma_start(out=wq_t[j][:], in_=wq_flat[:, :, 4 * BANK * j : 4 * BANK * (j + 1)].bitcast(I32))
 
+        def load_scales(plane, scales, passes):
+            for quad in range(QUADRANTS):
+                nc.sync.dma_start(
+                    out=plane[:].bitcast(I32)[32 * quad : 32 * quad + 4 * passes, :],
+                    in_=scales.bitcast(I32)[:, 4 * quad : 4 * quad + 4, :],
+                )
+
         load_hq(0)
         load_wq(0)
-        w_sc_words = w_sc[:].bitcast(I32)
-        for qd in range(4):
-            nc.sync.dma_start(
-                out=q_sc[:].bitcast(I32)[32 * qd : 32 * qd + 4, :], in_=wq_scales.bitcast(I32)[0, 4 * qd : 4 * qd + 4, :]
-            )
+        load_scales(q_sc, wq_scales, 1)
         load_wq(1)
         load_hq(1)
         load_wq(2)
         load_wq(3)
         load_hp(0)
-        for qd in range(4):
-            nc.sync.dma_start(
-                out=w_sc_words[32 * qd : 32 * qd + 8, :], in_=wp_scales.bitcast(I32)[:, 4 * qd : 4 * qd + 4, :]
-            )
+        load_scales(p_sc, wp_scales, 2)
         load_wp(0)
-        load_hq(2)
         load_wp(1)
-        load_hp(1)
+        load_hq(2)
         load_wp(2)
         load_wp(3)
+        load_hp(1)
         nc.sync.dma_start(out=g_row[0:1, :], in_=g.rearrange("(o v) -> o v", o=1))
         load_hq(3)
-        for i in (2, 3):
-            load_hp(i)
-        e_sc_words = e_sc[:].bitcast(I32)
-        for qd in range(4):
-            nc.sync.dma_start(
-                out=e_sc_words[32 * qd : 32 * qd + 16, :], in_=e_scales.bitcast(I32)[:, 4 * qd : 4 * qd + 4, :]
-            )
-        e_t = {}
-        for k in range(4):
+        load_hp(2)
+        load_hp(3)
+        load_scales(e_sc, e_scales, 4)
+        for k in range(V // K_PASS):
             e_t[k] = keep.tile([P, E], I32, name="e%d" % k, align_bytes=256)
             nc.sync.dma_start(out=e_t[k][:], in_=e_flat[:, k, :].bitcast(I32))
 
-        hpc, hps, hqc, hqs = {}, {}, {}, {}
+        g_sb = keep.tile([P, V], BF16, name="g_sb", align_bytes=64)
 
-        gp, gq = {}, {}
+        def g_turn(j):
+            t, b = take()
+            nc.tensor.matmul(t[:], lhsT=ones[:], rhs=g_row[:, BANK * j : BANK * (j + 1)], start=True, stop=True)
+            nc.scalar.copy(
+                out=g_sb[:, BANK * j : BANK * (j + 1)].rearrange("p (u q e) -> p u q e", u=2, e=2), in_=upe(t[:])
+            )
+            give(b)
 
-        def hp_turn(i, b=None):
-            t = bank(b)
+        gp, gq, hpc, hps, hqc, hqs = {}, {}, {}, {}, {}, {}
+
+        def hp_turn(i):
+            t, b = take()
             words = xp[i][:].bitcast(F32)
             for k in range(2):
                 for u in range(2):
                     c = (2 * k + u) * P
                     nc.tensor.transpose(t[:, c : c + P], words[:, 256 * k + u : 256 * (k + 1) : 2], ident[:])
-            gp[i] = hpool.tile([P, 4 * 256], BF16, name="gp", align_bytes=64)
-            nc.scalar.copy(
-                out=gp[i][:].bitcast(F32).rearrange("p (g r u) -> p g r u", g=2, u=2),
-                in_=t[:].rearrange("p (g u r) -> p g r u", g=2, u=2),
-            )
+            gp[i] = work.tile([P, 2 * BANK], BF16, name="gp", align_bytes=64)
+            nc.scalar.copy(out=as_words(gp[i][:], 2), in_=interleaved(t[:], 2))
+            give(b)
 
-        def hq_turn(i, b=None):
-            t = bank(b)
+        def hq_turn(i):
+            t, b = take()
             words = xq[i][:].bitcast(F32)
             for u in range(2):
                 nc.tensor.transpose(t[:, u * P : (u + 1) * P], words[:, u:256:2], ident[:])
-            gq[i] = hpool.tile([P, 4 * 128], BF16, name="gq", align_bytes=64)
-            nc.scalar.copy(
-                out=gq[i][:].bitcast(F32).rearrange("p (r u) -> p r u", u=2),
-                in_=t[:, 0:256].rearrange("p (u r) -> p r u", u=2),
-            )
+            gq[i] = work.tile([P, BANK], BF16, name="gq", align_bytes=64)
+            nc.scalar.copy(out=as_words(gq[i][:], 1), in_=interleaved(t[:, 0:256], 1))
+            give(b)
 
         def hp_quant(i):
-            hpc[i] = keep.tile([P, 256], U32, name="hpc%d" % i, align_bytes=64)
-            hps[i] = keep.tile([P, 256], U8, name="hps%d" % i, align_bytes=64)
+            hpc[i] = keep.tile([P, 2 * P], U32, name="hpc%d" % i, align_bytes=64)
+            hps[i] = keep.tile([P, 2 * P], U8, name="hps%d" % i, align_bytes=64)
             nc.vector.quantize_mx(out=hpc[i][:].bitcast(FP8X4), scales=hps[i][:], in_=gp[i][:])
 
         def hq_quant(i):
-            hqc[i] = keep.tile([P, 128], U32, name="hqc%d" % i, align_bytes=64)
-            hqs[i] = keep.tile([P, 128], U8, name="hqs%d" % i, align_bytes=64)
+            hqc[i] = keep.tile([P, P], U32, name="hqc%d" % i, align_bytes=64)
+            hqs[i] = keep.tile([P, P], U8, name="hqs%d" % i, align_bytes=64)
             nc.vector.quantize_mx(out=hqc[i][:].bitcast(FP8X4), scales=hqs[i][:], in_=gq[i][:])
 
         st = {}
 
-        def open_tile(i):
-            s = {}
-            s["ep"] = soft.tile([P, V], F32, name="ep", align_bytes=64)
-            s["eq"] = soft.tile([P, V], F32, name="eq", align_bytes=64)
-            s["mx"] = keep.tile([P, 8], F32, name="mx%d" % i)
-            s["nm"] = keep.tile([P, 2], F32, name="nm%d" % i)
-            s["zs"] = keep.tile([P, 8], F32, name="zs%d" % i)
-            for n in ("zt", "rz"):
-                s[n] = keep.tile([P, 2], F32, name="%s%d" % (n, i))
-            for n in ("sc", "r4", "r2", "bt", "nd", "c", "rc", "al"):
-                s[n] = keep.tile([P, 1], F32, name="%s%d" % (n, i))
-            s["zp"], s["zq"] = {}, {}
-            st[i] = s
+        def state(i):
+            if i not in st:
+                s = {"z": {}}
+                s["exp"] = [
+                    soft.tile([P, V], F32, name="ep", align_bytes=64),
+                    soft.tile([P, V], F32, name="eq", align_bytes=64),
+                ]
+                s["mx"] = keep.tile([P, 2 * BLOCKS], F32, name="mx%d" % i)
+                s["nm"] = keep.tile([P, 2], F32, name="nm%d" % i)
+                s["zs"] = keep.tile([P, 2 * BLOCKS], F32, name="zs%d" % i)
+                s["zt"] = keep.tile([P, 2], F32, name="zt%d" % i)
+                s["rz"] = keep.tile([P, 2], F32, name="rz%d" % i)
+                for n in ("sc", "r4", "r2", "bt", "nd", "c", "rc", "al"):
+                    s[n] = keep.tile([P, 1], F32, name="%s%d" % (n, i))
+                st[i] = s
+            return st[i]
 
-        def mm_p(i, j, b=None):
-            z = bank(b)
+        def mm_p(i, j):
+            z, b = take()
             for k in range(2):
                 nc.tensor.matmul_mx(
                     out=z[:],
                     lhsT=hpc[i][:, P * k : P * (k + 1)].bitcast(FP8X4),
                     lhsT_scale=hps[i][:, P * k : P * (k + 1)],
                     rhs=wp_t[j][:, k, :].bitcast(FP8X4),
-                    rhs_scale=w_sc[4 * k : P, BANK * j : BANK * (j + 1)],
+                    rhs_scale=p_sc[4 * k : P, BANK * j : BANK * (j + 1)],
                     start=(k == 0),
                     stop=(k == 1),
                 )
-            st[i]["zp"][j] = z
+            state(i)["z"][P_SIDE, j] = (z, b)
 
-        def mm_q(i, j, b=None):
-            z = bank(b)
+        def mm_q(i, j):
+            z, b = take()
             nc.tensor.matmul_mx(
                 out=z[:],
                 lhsT=hqc[i][:].bitcast(FP8X4),
@@ -202,59 +211,56 @@ def tile_spectrkseqresidualexpectedembedding_x2_kernel(
                 start=True,
                 stop=True,
             )
-            st[i]["zq"][j] = z
+            state(i)["z"][Q_SIDE, j] = (z, b)
 
-        def vmax(i, which, j):
+        def vmax(i, side, j):
             s = st[i]
-            c = 4 * which + j
-            z = s["zp" if which == 0 else "zq"][j]
-            nc.vector.tensor_reduce(out=s["mx"][:, c : c + 1], in_=z[:], axis=AX.X, op=ALU.max)
+            c = BLOCKS * side + j
+            nc.vector.tensor_reduce(out=s["mx"][:, c : c + 1], in_=s["z"][side, j][0][:], axis=AX.X, op=ALU.max)
 
-        def vmax_all(i, which):
+        def vmax_all(i, side):
             s = st[i]
             nc.vector.tensor_reduce(
-                out=s["nm"][:, which : which + 1],
-                in_=s["mx"][:, 4 * which : 4 * which + 4],
+                out=s["nm"][:, side : side + 1],
+                in_=s["mx"][:, BLOCKS * side : BLOCKS * (side + 1)],
                 axis=AX.X,
                 op=ALU.max,
                 negate=True,
             )
 
-        def zcopy(i, which, j):
+        def zcopy(i, side, j):
             s = st[i]
-            if j == 0:
-                s["zb", which] = work.tile([P, V], BF16, name="zb", align_bytes=64)
-                s["zm", which] = work.tile([P, V // 2], BF16, name="zm", align_bytes=64)
-            z = s["zp" if which == 0 else "zq"][j]
-            nc.scalar.copy(out=s["zb", which][:, BANK * j : BANK * (j + 1)], in_=z[:])
+            if ("zb", side) not in s:
+                s["zb", side] = work.tile([P, V], BF16, name="zb", align_bytes=64)
+                s["zm", side] = work.tile([P, V // 2], BF16, name="zm", align_bytes=64)
+            nc.scalar.copy(out=s["zb", side][:, BANK * j : BANK * (j + 1)], in_=s["z"][side, j][0][:])
 
-        def fold(i, which, step):
+        def fold(i, side, step):
             s = st[i]
-            zb, zm = s["zb", which], s["zm", which]
+            src, dst = (s["zb", side], s["zm", side]) if step % 2 == 0 else (s["zm", side], s["zb", side])
             w = V >> (step + 1)
-            src, dst = (zb, zm) if step % 2 == 0 else (zm, zb)
             nc.vector.tensor_tensor(out=dst[:, 0:w], in0=src[:, 0:w], in1=src[:, w : 2 * w], op=ALU.max)
 
-        def fold_end(i, which, step):
+        def fold_end(i, side, step):
             s = st[i]
-            src = s["zb", which] if step % 2 == 0 else s["zm", which]
+            src = s["zb", side] if step % 2 == 0 else s["zm", side]
             nc.vector.tensor_reduce(
-                out=s["nm"][:, which : which + 1], in_=src[:, 0 : V >> step], axis=AX.X, op=ALU.max, negate=True
+                out=s["nm"][:, side : side + 1], in_=src[:, 0 : V >> step], axis=AX.X, op=ALU.max, negate=True
             )
 
-        def exps(i, which, j):
+        def exps(i, side, j):
             s = st[i]
-            z = s["zp" if which == 0 else "zq"][j]
-            dst = s["ep" if which == 0 else "eq"]
-            c = 4 * which + j
+            z, b = s["z"][side, j]
+            c = BLOCKS * side + j
             nc.scalar.activation(
-                out=dst[:, BANK * j : BANK * (j + 1)].rearrange("p (u q e) -> p u q e", u=2, e=2),
-                in_=z[:].rearrange("p (q u e) -> p u q e", u=2, e=2),
+                out=s["exp"][side][:, BANK * j : BANK * (j + 1)].rearrange("p (u q e) -> p u q e", u=2, e=2),
+                in_=upe(z[:]),
                 func=ACT.Exp,
-                bias=s["nm"][:, which : which + 1],
+                bias=s["nm"][:, side : side + 1],
                 scale=1.0,
                 accum_out=s["zs"][:, c : c + 1],
             )
+            give(b)
 
         def sums(i):
             s = st[i]
@@ -265,13 +271,18 @@ def tile_spectrkseqresidualexpectedembedding_x2_kernel(
         def inv_sums(i):
             s = st[i]
             nc.vector.reciprocal(out=s["rz"][:], in_=s["zt"][:])
-            nc.scalar.activation(out=s["r4"][:], in_=s["rz"][:, 0:1], func=ACT.Copy, scale=0.25)
-            nc.scalar.activation(out=s["r2"][:], in_=s["rz"][:, 0:1], func=ACT.Copy, scale=-0.5)
+            nc.scalar.activation(out=s["r4"][:], in_=s["rz"][:, P_SIDE : P_SIDE + 1], func=ACT.Copy, scale=0.25)
+            nc.scalar.activation(out=s["r2"][:], in_=s["rz"][:, P_SIDE : P_SIDE + 1], func=ACT.Copy, scale=-0.5)
 
         def ratio(i):
             s = st[i]
             nc.vector.tensor_scalar(
-                out=s["sc"][:], in0=s["zt"][:, 0:1], scalar1=2.0, scalar2=s["rz"][:, 1:2], op0=ALU.mult, op1=ALU.mult
+                out=s["sc"][:],
+                in0=s["zt"][:, P_SIDE : P_SIDE + 1],
+                scalar1=2.0,
+                scalar2=s["rz"][:, Q_SIDE : Q_SIDE + 1],
+                op0=ALU.mult,
+                op1=ALU.mult,
             )
 
         def vmin(i):
@@ -280,9 +291,9 @@ def tile_spectrkseqresidualexpectedembedding_x2_kernel(
             s["a"] = work.tile([P, V], BF16, name="a", align_bytes=64)
             nc.vector.scalar_tensor_tensor(
                 out=s["m"][:],
-                in0=s["eq"][:],
+                in0=s["exp"][Q_SIDE][:],
                 scalar=s["sc"][:, 0:1],
-                in1=s["ep"][:],
+                in1=s["exp"][P_SIDE][:],
                 op0=ALU.mult,
                 op1=ALU.min,
                 accum_out=s["bt"][:, 0:1],
@@ -310,7 +321,7 @@ def tile_spectrkseqresidualexpectedembedding_x2_kernel(
                 out=s["al"][:],
                 in0=s["rc"][:],
                 scalar1=s["rc"][:, 0:1],
-                scalar2=s["rz"][:, 0:1],
+                scalar2=s["rz"][:, P_SIDE : P_SIDE + 1],
                 op0=ALU.mult,
                 op1=ALU.mult,
             )
@@ -321,7 +332,7 @@ def tile_spectrkseqresidualexpectedembedding_x2_kernel(
                 out=s["m"][:, lo:hi],
                 in0=s["m"][:, lo:hi],
                 scalar=s["nd"][:, 0:1],
-                in1=s["ep"][:, lo:hi],
+                in1=s["exp"][P_SIDE][:, lo:hi],
                 op0=ALU.mult,
                 op1=ALU.add,
             )
@@ -344,28 +355,28 @@ def tile_spectrkseqresidualexpectedembedding_x2_kernel(
             nc.scalar.activation(out=s["d1"][:], in_=ident[:], func=ACT.Copy, scale=s["al"][:, 0:1])
             nc.scalar.activation(out=s["d2"][:], in_=s["d1"][:], func=ACT.Copy, scale=s["nd"][:, 0:1])
 
-        def mm_sub(i, k, b=None):
+        def mm_sub(i, k):
             s = st[i]
-            t = bank(b)
-            s["r", k] = t
+            t, b = take()
+            s["r", k] = (t, b)
             cols = slice(BANK * k, BANK * (k + 1))
-            nc.tensor.matmul(t[:], lhsT=s["d1"][:], rhs=s["ep"][:, cols], start=True, stop=False)
+            nc.tensor.matmul(t[:], lhsT=s["d1"][:], rhs=s["exp"][P_SIDE][:, cols], start=True, stop=False)
             nc.tensor.matmul(t[:], lhsT=s["d2"][:], rhs=s["m"][:, cols], start=False, stop=True)
 
         def vgain_t(i, k):
             s = st[i]
+            t, b = s["r", k]
             cols = slice(BANK * k, BANK * (k + 1))
-            nc.vector.tensor_tensor(out=s["a"][:, cols], in0=s["r", k][:], in1=g_sb[:, cols], op=ALU.mult)
+            nc.vector.tensor_tensor(out=s["a"][:, cols], in0=t[:], in1=g_sb[:, cols], op=ALU.mult)
+            give(b)
 
-        def open_a(i):
+        def a_turn(i, k0, nk):
             s = st[i]
-            s["ga"] = work.tile([P, 4 * BANK], BF16, name="ga", align_bytes=64)
-            s["ac"] = work.tile([P, BANK], U32, name="ac", align_bytes=64)
-            s["as"] = work.tile([P, BANK], U8, name="as_", align_bytes=64)
-
-        def a_turn(i, k0, nk, b=None):
-            s = st[i]
-            t = bank(b)
+            if "ga" not in s:
+                s["ga"] = work.tile([P, V], BF16, name="ga", align_bytes=64)
+                s["ac"] = work.tile([P, BANK], U32, name="ac", align_bytes=64)
+                s["as"] = work.tile([P, BANK], U8, name="as", align_bytes=64)
+            t, b = take()
             words = s["a"][:].bitcast(F32)
             for k in range(nk):
                 for u in range(2):
@@ -373,9 +384,9 @@ def tile_spectrkseqresidualexpectedembedding_x2_kernel(
                     w = 256 * (k0 + k) + P * u
                     nc.tensor.transpose(t[:, c : c + P], words[:, w : w + P], ident[:])
             nc.scalar.copy(
-                out=s["ga"][:, BANK * k0 : BANK * (k0 + nk)].bitcast(F32).rearrange("p (g r u) -> p g r u", g=nk, u=2),
-                in_=t[:, 0 : 256 * nk].rearrange("p (g u r) -> p g r u", g=nk, u=2),
+                out=as_words(s["ga"][:, BANK * k0 : BANK * (k0 + nk)], nk), in_=interleaved(t[:, 0 : 256 * nk], nk)
             )
+            give(b)
 
         def a_quant(i, k0, nk):
             s = st[i]
@@ -385,41 +396,45 @@ def tile_spectrkseqresidualexpectedembedding_x2_kernel(
                 in_=s["ga"][:, BANK * k0 : BANK * (k0 + nk)],
             )
 
-        def open_out(i, b0=None, b1=None):
-            st[i]["o"] = [bank(b0), bank(b1)]
-
-        def mm_out(i, k, order=(0, 1, 2, 3)):
+        def mm_out(i, k):
             s = st[i]
+            if "o" not in s:
+                s["o"] = [take(), take()]
             for h in range(2):
                 nc.tensor.matmul_mx(
-                    out=s["o"][h][:],
+                    out=s["o"][h][0][:],
                     lhsT=s["ac"][:, P * k : P * (k + 1)].bitcast(FP8X4),
                     lhsT_scale=s["as"][:, P * k : P * (k + 1)],
                     rhs=e_t[k][:, BANK * h : BANK * (h + 1)].bitcast(FP8X4),
                     rhs_scale=e_sc[4 * k : P, BANK * h : BANK * (h + 1)],
-                    start=(k == order[0]),
-                    stop=(k == order[3]),
+                    start=(k == 0),
+                    stop=(k == V // K_PASS - 1),
                 )
 
         ps = keep.tile([P, 2, N], U8, name="ps", align_bytes=256)
 
-        def open_evac(i):
+        def read_out(i, h):
             s = st[i]
-            s["of"] = work.tile([P, E], F32, name="of", align_bytes=64)
-            s["ob"] = work.tile([P, E], BF16, name="ob", align_bytes=64)
-            s["pc"] = work.tile([P, 2, P], U32, name="pc", align_bytes=64)
-            s["go"] = work.tile([P, 2 * BANK], BF16, name="go", align_bytes=64)
+            if "of" not in s:
+                s["of"] = work.tile([P, E], F32, name="of", align_bytes=64)
+                s["ob"] = work.tile([P, E], BF16, name="ob", align_bytes=64)
+                s["pc"] = work.tile([P, 2, P], U32, name="pc", align_bytes=64)
+                s["go"] = work.tile([P, 2 * BANK], BF16, name="go", align_bytes=64)
+                s["left"] = {0: 2, 1: 2}
+            s["left"][h] -= 1
+            if s["left"][h] == 0:
+                give(s["o"][h][1])
+            return s["o"][h][0]
 
         def evac_b(i, h, copy):
-            s = st[i]
+            o = read_out(i, h)
             copy(
-                out=s["ob"][:, BANK * h : BANK * (h + 1)].rearrange("p (u q e) -> p u q e", u=2, e=2),
-                in_=s["o"][h][:].rearrange("p (q u e) -> p u q e", u=2, e=2),
+                out=st[i]["ob"][:, BANK * h : BANK * (h + 1)].rearrange("p (u q e) -> p u q e", u=2, e=2), in_=upe(o[:])
             )
 
         def evac_f(i, h, copy):
-            s = st[i]
-            copy(out=s["of"][:, BANK * h : BANK * (h + 1)], in_=s["o"][h][:])
+            o = read_out(i, h)
+            copy(out=st[i]["of"][:, BANK * h : BANK * (h + 1)], in_=o[:])
 
         def store_f(i):
             nc.sync.dma_start(out=out[P * i : P * (i + 1), :], in_=st[i]["of"][:])
@@ -428,17 +443,15 @@ def tile_spectrkseqresidualexpectedembedding_x2_kernel(
             cols = slice(BANK * h, BANK * (h + 1))
             queue.dma_start(out=out[P * i : P * (i + 1), cols], in_=st[i]["of"][:, cols])
 
-        def o_turn(i, k0, nk, copy, b=None):
+        def o_turn(i, k0, nk, copy):
             s = st[i]
-            t = bank(b)
+            t, b = take()
             words = s["ob"][:].bitcast(F32)
             for c in range(2 * nk):
                 w = 256 * k0 + P * c
                 nc.tensor.transpose(t[:, P * c : P * (c + 1)], words[:, w : w + P], ident[:])
-            copy(
-                out=s["go"][:, BANK * k0 : BANK * (k0 + nk)].bitcast(F32).rearrange("p (g r u) -> p g r u", g=nk, u=2),
-                in_=t[:, 0 : 256 * nk].rearrange("p (g u r) -> p g r u", g=nk, u=2),
-            )
+            copy(out=as_words(s["go"][:, BANK * k0 : BANK * (k0 + nk)], nk), in_=interleaved(t[:, 0 : 256 * nk], nk))
+            give(b)
 
         def o_quant(i, k):
             s = st[i]
@@ -448,305 +461,226 @@ def tile_spectrkseqresidualexpectedembedding_x2_kernel(
                 in_=s["go"][:, BANK * k : BANK * (k + 1)],
             )
 
-        pc_dram = out_words.rearrange("g p m t -> p g (m t)")
-
         def store_codes(i):
             nc.sync.dma_start(
-                out=pc_dram[:, :, 4 * P * i : 4 * P * (i + 1)].bitcast(I32),
+                out=out_words.rearrange("g p m t -> p g (m t)")[:, :, 4 * P * i : 4 * P * (i + 1)].bitcast(I32),
                 in_=st[i]["pc"][:].bitcast(I32),
             )
 
         def store_scales():
-            ps_words = ps[:].rearrange("p g m -> p (g m)").bitcast(I32)
-            for qd in range(4):
+            rows = ps[:].rearrange("p g m -> p (g m)").bitcast(I32)
+            for quad in range(QUADRANTS):
                 nc.sync.dma_start(
-                    out=out_scales.bitcast(I32)[:, 4 * qd : 4 * qd + 4, :].rearrange("g r m -> r g m"),
-                    in_=ps_words[32 * qd : 32 * qd + 4, :].rearrange("r (g m) -> r g m", g=2),
+                    out=out_scales.bitcast(I32)[:, 4 * quad : 4 * quad + 4, :].rearrange("g r m -> r g m"),
+                    in_=rows[32 * quad : 32 * quad + 4, :].rearrange("r (g m) -> r g m", g=2),
                 )
 
-        g_sb = keep.tile([P, V], BF16, name="g_sb", align_bytes=64)
-
-        def g_turn(j, b=None):
-            t = bank(b)
-            nc.tensor.matmul(t[:], lhsT=ones[:], rhs=g_row[:, BANK * j : BANK * (j + 1)], start=True, stop=True)
-            nc.scalar.copy(
-                out=g_sb[:, BANK * j : BANK * (j + 1)].rearrange("p (u q e) -> p u q e", u=2, e=2),
-                in_=t[:].rearrange("p (q u e) -> p u q e", u=2, e=2),
-            )
-
-        hq_turn(0, 0)
+        hq_turn(0)
+        hq_turn(1)
+        hp_turn(0)
         hq_quant(0)
-        open_tile(0)
-        mm_q(0, 1, 1)
-        hq_turn(1, 2)
-        mm_q(0, 2, 3)
-        mm_q(0, 0, 4)
-        hp_turn(0, 5)
-        mm_q(0, 3, 6)
-        hq_quant(1)
-        open_tile(1)
-        mm_q(1, 3, 7)
-        vmax(0, 1, 0)
-        vmax(0, 1, 1)
-        vmax(0, 1, 3)
-        vmax(0, 1, 2)
-        hq_turn(2, 0)
-        vmax_all(0, 1)
         hp_quant(0)
-        mm_q(1, 2, 2)
-        mm_p(0, 0, 5)
-        mm_q(1, 0, 0)
-        vmax(1, 1, 3)
-        exps(0, 1, 2)
-        exps(0, 1, 3)
-        vmax(1, 1, 2)
-        hp_turn(1, 3)
-        exps(0, 1, 0)
-        vmax(1, 1, 0)
-        exps(0, 1, 1)
-        mm_p(0, 1, 6)
-        vmax(0, 0, 0)
+        for j in range(4):
+            mm_q(0, j)
+        hq_turn(2)
+        for j in range(4):
+            mm_p(0, j)
+        for j in range(4):
+            vmax(0, Q_SIDE, j)
+        hq_quant(1)
+        vmax_all(0, Q_SIDE)
         hq_quant(2)
-        mm_p(0, 2, 3)
-        mm_p(0, 3, 4)
-        vmax(0, 0, 1)
-        g_turn(0, 1)
-        vmax(0, 0, 2)
-        vmax(0, 0, 3)
-        vmax_all(0, 0)
-        exps(0, 0, 3)
-        mm_q(1, 1, 1)
+        for j in range(4):
+            vmax(0, P_SIDE, j)
+        for j in range(4):
+            exps(0, Q_SIDE, j)
+        hp_turn(1)
+        for j in range(4):
+            mm_q(1, j)
+        vmax_all(0, P_SIDE)
+        for j in range(2):
+            vmax(1, Q_SIDE, j)
+        for j in range(4):
+            exps(0, P_SIDE, j)
+        hp_turn(2)
         hp_quant(1)
-        exps(0, 0, 0)
-        vmax(1, 1, 1)
-        vmax_all(1, 1)
-        mm_p(1, 0, 4)
-        vmax(1, 0, 0)
-        exps(0, 0, 2)
-        mm_p(1, 2, 5)
-        vmax(1, 0, 2)
-        exps(0, 0, 1)
+        for j in range(2, 4):
+            vmax(1, Q_SIDE, j)
+        for j in range(4):
+            mm_p(1, j)
+        vmax(1, P_SIDE, 0)
+        vmax_all(1, Q_SIDE)
+        for j in range(4):
+            exps(1, Q_SIDE, j)
         sums(0)
-        mm_p(1, 1, 3)
-        mm_p(1, 3, 6)
-        exps(1, 1, 3)
-        vmax(1, 0, 1)
-        exps(1, 1, 1)
-        hp_turn(2, 7)
+        for j in range(1, 3):
+            vmax(1, P_SIDE, j)
         inv_sums(0)
-        vmax(1, 0, 3)
+        vmax(1, P_SIDE, 3)
         ratio(0)
-        vmax_all(1, 0)
-        open_tile(2)
-        mm_q(2, 2, 1)
-        vmin(0)
-        mm_q(2, 1, 7)
+        hq_turn(3)
         hp_quant(2)
-        small_c(0)
-        exps(1, 0, 1)
-        exps(1, 1, 2)
+        hp_turn(3)
+        vmax_all(1, P_SIDE)
+        for j in range(4):
+            mm_p(2, j)
+        vmin(0)
+        vmax(2, P_SIDE, 0)
         small_nd(0)
-        hp_turn(3, 3)
-        mm_p(2, 3, 2)
-        exps(1, 1, 0)
-        mm_q(2, 0, 3)
-        exps(1, 0, 0)
-        vmax(2, 1, 1)
-        mm_p(2, 1, 0)
-        exps(1, 0, 3)
-        vmax(2, 1, 2)
-        exps(1, 0, 2)
-        vsub(0, 512, 1536)
-        vmax(2, 1, 0)
-        sums(1)
-        mm_p(2, 0, 4)
-        hp_quant(3)
+        small_c(0)
+        for j in range(1, 4):
+            vmax(2, P_SIDE, j)
         small_rc(0)
-        inv_sums(1)
-        vmax(2, 0, 1)
-        ratio(1)
-        hq_turn(3, 6)
-        mm_p(2, 2, 5)
+        vsub(0, 0, 1536)
+        for j in range(4):
+            exps(1, P_SIDE, j)
+        for j in range(4):
+            g_turn(j)
+        sums(1)
+        for j in range(4):
+            mm_q(2, j)
         small_al(0)
-        vmax(2, 0, 2)
-        g_turn(2, 6)
-        vmax(2, 0, 0)
-        g_turn(3, 6)
-        vmax(2, 0, 3)
-        vsub(0, 0, 512)
-        vmax_all(2, 0)
-        vmin(1)
-        mm_q(2, 3, 6)
-        exps(2, 0, 3)
-        g_turn(1, 2)
-        exps(2, 0, 0)
-        exps(2, 0, 2)
-        vgain(0, 1024, 1536)
-        small_nd(1)
-        diags(0)
-        vmax(2, 1, 3)
-        vsub(1, 0, 512)
-        vmax_all(2, 1)
-        exps(2, 1, 3)
-        open_tile(3)
-        mm_p(3, 0, 2)
-        mm_sub(0, 3, 4)
-        exps(2, 1, 2)
-        exps(2, 1, 1)
-        vgain(0, 0, 1024)
-        exps(2, 0, 1)
-        small_c(1)
-        vmax(3, 0, 0)
-        vsub(1, 512, 1536)
-        small_rc(1)
-        vgain_t(0, 3)
+        for j in range(4):
+            zcopy(2, Q_SIDE, j)
+        vmax_all(2, P_SIDE)
+        hp_quant(3)
+        vgain(0, 0, 1536)
+        fold(2, Q_SIDE, 0)
+        for j in range(4):
+            exps(2, P_SIDE, j)
         hq_quant(3)
-        mm_p(3, 1, 5)
-        mm_p(3, 2, 6)
-        vmax(3, 0, 1)
-        mm_p(3, 3, 1)
-        exps(2, 1, 0)
-        vmax(3, 0, 3)
-        mm_q(3, 3, 7)
-        vmax(3, 0, 2)
-        open_a(0)
-        a_turn(0, 0, 2, 0)
-        a_turn(0, 2, 2, 3)
+        inv_sums(1)
+        diags(0)
+        for step in range(1, 3):
+            fold(2, Q_SIDE, step)
+        for j in range(3):
+            mm_p(3, j)
+        ratio(1)
+        fold_end(2, Q_SIDE, 3)
+        for j in range(4):
+            exps(2, Q_SIDE, j)
+        vmin(1)
+        for j in range(2):
+            vmax(3, P_SIDE, j)
         sums(2)
-        mm_q(3, 1, 4)
-        vmax(3, 1, 3)
-        vmax_all(3, 0)
-        small_al(1)
+        mm_sub(0, 3)
+        vgain_t(0, 3)
+        a_turn(0, 0, 2)
         inv_sums(2)
-        a_quant(0, 0, 4)
-        mm_q(3, 2, 0)
+        mm_p(3, 3)
+        vmax(3, P_SIDE, 2)
+        small_c(1)
         ratio(2)
-        vmax(3, 1, 2)
-        exps(3, 0, 2)
-        mm_q(3, 0, 3)
-        vmax(3, 1, 1)
-        exps(3, 0, 1)
-        vmax(3, 1, 0)
-        diags(1)
-        vgain(1, 0, 1024)
-        mm_sub(1, 3, 6)
-        exps(3, 0, 3)
-        vmax_all(3, 1)
-        exps(3, 0, 0)
-        exps(3, 1, 1)
+        vmax(3, P_SIDE, 3)
+        a_turn(0, 2, 2)
+        for j in range(4):
+            mm_q(3, j)
+        small_rc(1)
+        for j in range(4):
+            zcopy(3, Q_SIDE, j)
         vmin(2)
-        vgain_t(1, 3)
-        open_out(0, 5, 1)
-        mm_out(0, 0)
-        exps(3, 1, 3)
-        exps(3, 1, 0)
-        vgain(1, 1024, 1536)
-        open_a(1)
-        a_turn(1, 0, 2, 2)
-        mm_out(0, 1)
-        mm_out(0, 2)
+        vmax_all(3, P_SIDE)
+        fold(3, Q_SIDE, 0)
+        a_quant(0, 0, 4)
+        fold(3, Q_SIDE, 1)
+        small_al(1)
+        small_nd(1)
         small_nd(2)
-        mm_out(0, 3)
-        exps(3, 1, 2)
-        a_turn(1, 2, 2, 4)
-        a_quant(1, 0, 2)
+        for j in range(4):
+            exps(3, P_SIDE, j)
         small_c(2)
-        sums(3)
-        open_evac(0)
-        evac_f(0, 0, nc.scalar.copy)
-        open_out(1, 7, 3)
-        mm_out(1, 0)
-        vsub(2, 0, 512)
+        fold(3, Q_SIDE, 2)
+        vsub(1, 0, 1536)
+        fold_end(3, Q_SIDE, 3)
         small_rc(2)
-        mm_out(1, 1)
-        inv_sums(3)
-        vsub(2, 512, 1024)
-        ratio(3)
-        a_quant(1, 2, 2)
-        mm_out(1, 2)
+        diags(1)
+        for k in range(4):
+            mm_out(0, k)
+        vgain(1, 0, 1536)
         small_al(2)
-        vmin(3)
+        for j in range(4):
+            exps(3, Q_SIDE, j)
+        mm_sub(1, 3)
+        vsub(2, 0, 1024)
         diags(2)
-        vgain(2, 0, 512)
-        vgain(2, 512, 1024)
-        mm_sub(2, 2, 2)
-        small_nd(3)
-        small_c(3)
-        vgain_t(2, 2)
-        evac_b(0, 1, nc.scalar.copy)
+        a_turn(1, 0, 2)
+        sums(3)
         evac_f(0, 1, nc.scalar.copy)
-        mm_out(1, 3)
-        open_evac(1)
-        evac_f(1, 0, nc.scalar.copy)
-        open_a(2)
-        a_turn(2, 0, 2, 6)
-        vsub(3, 0, 1024)
-        mm_sub(2, 3, 0)
         evac_b(0, 0, nc.scalar.copy)
-        small_rc(3)
+        vgain_t(1, 3)
+        evac_b(0, 1, nc.scalar.copy)
+        inv_sums(3)
+        vgain(2, 0, 1024)
+        mm_sub(2, 2)
+        a_turn(1, 2, 2)
+        a_turn(2, 0, 2)
+        mm_sub(2, 3)
+        ratio(3)
+        a_quant(1, 0, 2)
+        evac_f(0, 0, nc.scalar.copy)
+        vmin(3)
         a_quant(2, 0, 2)
-        evac_f(1, 1, nc.scalar.copy)
-        evac_b(1, 0, nc.scalar.copy)
-        small_al(3)
-        evac_b(1, 1, nc.scalar.copy)
-        o_turn(0, 0, 2, nc.scalar.copy, 4)
-        vsub(3, 1024, 1536)
-        vgain_t(2, 3)
-        open_out(2, 1, 2)
-        mm_out(2, 0)
-        vgain(3, 1024, 1536)
-        a_turn(2, 2, 2, 6)
-        o_turn(1, 0, 2, nc.scalar.copy, 5)
-        mm_out(2, 1)
-        vgain(3, 512, 1024)
-        vgain(3, 0, 512)
-        open_a(3)
-        a_turn(3, 1, 1, 7)
+        small_c(3)
+        a_quant(1, 2, 2)
         store_f(0)
+        o_turn(0, 0, 2, nc.scalar.copy)
+        small_rc(3)
+        small_nd(3)
+        for k in range(2):
+            mm_out(1, k)
+        for k in range(2, 4):
+            vgain_t(2, k)
+        vsub(3, 0, 2048)
+        a_turn(2, 2, 2)
+        small_al(3)
+        for k in range(2, 4):
+            mm_out(1, k)
+        evac_b(1, 0, nc.scalar.copy)
         a_quant(2, 2, 2)
-        a_turn(3, 2, 1, 3)
-        o_quant(1, 1)
-        a_turn(3, 0, 1, 0)
+        for k in range(3):
+            mm_out(2, k)
+        for k in range(4):
+            vgain(3, BANK * k, BANK * (k + 1))
+        evac_f(1, 0, nc.scalar.copy)
+        evac_b(1, 1, nc.scalar.copy)
+        evac_f(1, 1, nc.scalar.copy)
+        a_turn(3, 0, 1)
+        o_turn(1, 0, 2, nc.scalar.copy)
+        a_turn(3, 1, 1)
         store_f(1)
-        vsub(3, 1536, 2048)
-        a_quant(3, 1, 1)
-        mm_out(2, 2)
-        a_quant(3, 0, 1)
         mm_out(2, 3)
-        vgain(3, 1536, 2048)
-        o_quant(0, 0)
-        open_out(3, 4, 6)
-        mm_out(3, 0)
-        open_evac(2)
-        evac_b(2, 1, nc.scalar.copy)
-        o_quant(0, 1)
-        a_turn(3, 3, 1, 5)
+        a_turn(3, 2, 1)
+        a_quant(3, 0, 1)
+        for k in range(2):
+            o_quant(1, k)
         evac_f(2, 1, nc.scalar.copy)
+        a_quant(3, 1, 1)
+        for k in range(2):
+            o_quant(0, k)
         a_quant(3, 2, 1)
-        evac_b(2, 0, nc.scalar.copy)
-        o_quant(1, 0)
+        store_codes(1)
+        store_codes(0)
+        a_turn(3, 3, 1)
+        for h in range(2):
+            evac_b(2, h, nc.scalar.copy)
         a_quant(3, 3, 1)
         evac_f(2, 0, nc.vector.tensor_copy)
-        store_codes(0)
-        mm_out(3, 1)
-        mm_out(3, 2)
-        mm_out(3, 3)
-        open_evac(3)
+        for k in range(4):
+            mm_out(3, k)
         evac_b(3, 1, nc.scalar.copy)
-        store_codes(1)
         evac_b(3, 0, nc.vector.tensor_copy)
-        o_turn(2, 0, 2, nc.scalar.copy, 7)
         evac_f(3, 0, nc.vector.tensor_copy)
-        o_turn(3, 0, 1, nc.vector.tensor_copy, 3)
-        o_quant(2, 1)
+        o_turn(2, 0, 2, nc.scalar.copy)
         store_f(2)
-        o_quant(2, 0)
-        o_turn(3, 1, 1, nc.scalar.copy, 0)
-        evac_f(3, 1, nc.scalar.copy)
-        o_quant(3, 0)
+        o_turn(3, 0, 1, nc.vector.tensor_copy)
         store_f_half(3, 0, nc.sync)
+        for k in range(2):
+            o_quant(2, k)
         store_codes(2)
-        o_quant(3, 1)
+        o_turn(3, 1, 1, nc.scalar.copy)
+        for k in range(2):
+            o_quant(3, k)
+        evac_f(3, 1, nc.scalar.copy)
+        store_codes(3)
         store_f_half(3, 1, nc.scalar)
         store_scales()
-        store_codes(3)

from contextlib import ExitStack

import concourse.mybir as mybir
from concourse.masks import make_identity

N, D, Q, V, E = 512, 1024, 512, 2048, 1024

FLOPS = 2 * N * V * (D + Q) + 2 * N * V * E

F32 = mybir.dt.float32
BF16 = mybir.dt.bfloat16
I32 = mybir.dt.int32
U32 = mybir.dt.uint32
U8 = mybir.dt.uint8
FP8X4 = mybir.dt.float8_e4m3fn_x4
ALU = mybir.AluOpType
ACT = mybir.ActivationFunctionType
AX = mybir.AxisListType

P = 128
K_PASS = 512
BANK = 512
BLOCKS = V // BANK
QUADRANTS = 4
P_SIDE, Q_SIDE = 0, 1


def upe(bank):
    return bank.rearrange("p (q u e) -> p u q e", u=2, e=2)


def interleaved(turned, groups):
    return turned.rearrange("p (g u r) -> p g r u", g=groups, u=2)


def as_words(rows, groups):
    return rows.bitcast(F32).rearrange("p (g r u) -> p g r u", g=groups, u=2)


def tile_spectrkseqresidualexpectedembedding_x2_kernel(
    tc, hp, wp_words, wp_scales, hq, wq_words, wq_scales, g, e_words, e_scales, out, out_words, out_scales
):
    nc = tc.nc

    with ExitStack() as ctx:
        keep = ctx.enter_context(tc.tile_pool(name="keep", bufs=1))
        soft = ctx.enter_context(tc.tile_pool(name="soft", bufs=4))
        work = ctx.enter_context(tc.tile_pool(name="work", bufs=2))
        psum = ctx.enter_context(tc.psum_pool(name="psum", bufs=1))
        ctx.enter_context(tc.manual_schedule())

        banks = {"free": list(range(8))}

        def take():
            b = banks["free"][0]
            banks["free"] = banks["free"][1:]
            return psum.tile([P, BANK], F32, name="bank%d" % b, tag="bank%d" % b), b

        def give(b):
            banks["free"] = banks["free"] + [b]

        q_sc = keep.tile([P, V], U8, name="q_sc", align_bytes=256)
        nc.vector.memset(q_sc[:].bitcast(I32), 0)
        p_sc = keep.tile([P, V], U8, name="p_sc", align_bytes=256)
        nc.vector.memset(p_sc[:].bitcast(I32), 0)
        g_row = keep.tile([P, V], BF16, name="g_row", align_bytes=256)
        nc.vector.memset(g_row[:].bitcast(I32), 0)
        e_sc = keep.tile([P, E], U8, name="e_sc", align_bytes=256)
        nc.vector.memset(e_sc[:].bitcast(I32), 0)
        ident = keep.tile([P, P], F32, name="ident", align_bytes=64)
        make_identity(nc, ident[:])
        ones = keep.tile([P, P], BF16, name="ones", align_bytes=64)
        nc.scalar.activation(out=ones[:], in_=ident[:], func=ACT.Exp, scale=0.0)

        xp, xq, wp_t, wq_t, e_t = {}, {}, {}, {}, {}

        def load_hp(i):
            xp[i] = keep.tile([P, D], BF16, name="xp%d" % i, align_bytes=256)
            nc.sync.dma_start(out=xp[i][:], in_=hp[P * i : P * (i + 1), :])

        def load_hq(i):
            xq[i] = keep.tile([P, Q], BF16, name="xq%d" % i, align_bytes=256)
            nc.sync.dma_start(out=xq[i][:], in_=hq[P * i : P * (i + 1), :])

        wp_flat = wp_words.rearrange("g p n t -> p g (n t)")
        wq_flat = wq_words.rearrange("g p n t -> p g (n t)")
        e_flat = e_words.rearrange("g p n t -> p g (n t)")

        def load_wp(j):
            wp_t[j] = keep.tile([P, 2, BANK], I32, name="wp%d" % j, align_bytes=256)
            nc.sync.dma_start(out=wp_t[j][:], in_=wp_flat[:, :, 4 * BANK * j : 4 * BANK * (j + 1)].bitcast(I32))

        def load_wq(j):
            wq_t[j] = keep.tile([P, 1, BANK], I32, name="wq%d" % j, align_bytes=256)
            nc.sync.dma_start(out=wq_t[j][:], in_=wq_flat[:, :, 4 * BANK * j : 4 * BANK * (j + 1)].bitcast(I32))

        def load_scales(plane, scales, passes):
            for quad in range(QUADRANTS):
                nc.sync.dma_start(
                    out=plane[:].bitcast(I32)[32 * quad : 32 * quad + 4 * passes, :],
                    in_=scales.bitcast(I32)[:, 4 * quad : 4 * quad + 4, :],
                )

        load_hq(0)
        load_wq(0)
        load_scales(q_sc, wq_scales, 1)
        load_wq(1)
        load_hq(1)
        load_wq(2)
        load_wq(3)
        load_hp(0)
        load_scales(p_sc, wp_scales, 2)
        load_wp(0)
        load_wp(1)
        load_hq(2)
        load_wp(2)
        load_wp(3)
        load_hp(1)
        nc.sync.dma_start(out=g_row[0:1, :], in_=g.rearrange("(o v) -> o v", o=1))
        load_hq(3)
        load_hp(2)
        load_hp(3)
        load_scales(e_sc, e_scales, 4)
        for k in range(V // K_PASS):
            e_t[k] = keep.tile([P, E], I32, name="e%d" % k, align_bytes=256)
            nc.sync.dma_start(out=e_t[k][:], in_=e_flat[:, k, :].bitcast(I32))

        g_sb = keep.tile([P, V], BF16, name="g_sb", align_bytes=64)

        def g_turn(j):
            t, b = take()
            nc.tensor.matmul(t[:], lhsT=ones[:], rhs=g_row[:, BANK * j : BANK * (j + 1)], start=True, stop=True)
            nc.scalar.copy(
                out=g_sb[:, BANK * j : BANK * (j + 1)].rearrange("p (u q e) -> p u q e", u=2, e=2), in_=upe(t[:])
            )
            give(b)

        gp, gq, hpc, hps, hqc, hqs = {}, {}, {}, {}, {}, {}

        def hp_turn(i):
            t, b = take()
            words = xp[i][:].bitcast(F32)
            for k in range(2):
                for u in range(2):
                    c = (2 * k + u) * P
                    nc.tensor.transpose(t[:, c : c + P], words[:, 256 * k + u : 256 * (k + 1) : 2], ident[:])
            gp[i] = work.tile([P, 2 * BANK], BF16, name="gp", align_bytes=64)
            nc.scalar.copy(out=as_words(gp[i][:], 2), in_=interleaved(t[:], 2))
            give(b)

        def hq_turn(i):
            t, b = take()
            words = xq[i][:].bitcast(F32)
            for u in range(2):
                nc.tensor.transpose(t[:, u * P : (u + 1) * P], words[:, u:256:2], ident[:])
            gq[i] = work.tile([P, BANK], BF16, name="gq", align_bytes=64)
            nc.scalar.copy(out=as_words(gq[i][:], 1), in_=interleaved(t[:, 0:256], 1))
            give(b)

        def hp_quant(i):
            hpc[i] = keep.tile([P, 2 * P], U32, name="hpc%d" % i, align_bytes=64)
            hps[i] = keep.tile([P, 2 * P], U8, name="hps%d" % i, align_bytes=64)
            nc.vector.quantize_mx(out=hpc[i][:].bitcast(FP8X4), scales=hps[i][:], in_=gp[i][:])

        def hq_quant(i):
            hqc[i] = keep.tile([P, P], U32, name="hqc%d" % i, align_bytes=64)
            hqs[i] = keep.tile([P, P], U8, name="hqs%d" % i, align_bytes=64)
            nc.vector.quantize_mx(out=hqc[i][:].bitcast(FP8X4), scales=hqs[i][:], in_=gq[i][:])

        st = {}

        def state(i):
            if i not in st:
                s = {"z": {}}
                s["exp"] = [
                    soft.tile([P, V], F32, name="ep", align_bytes=64),
                    soft.tile([P, V], F32, name="eq", align_bytes=64),
                ]
                s["mx"] = keep.tile([P, 2 * BLOCKS], F32, name="mx%d" % i)
                s["nm"] = keep.tile([P, 2], F32, name="nm%d" % i)
                s["zs"] = keep.tile([P, 2 * BLOCKS], F32, name="zs%d" % i)
                s["zt"] = keep.tile([P, 2], F32, name="zt%d" % i)
                s["rz"] = keep.tile([P, 2], F32, name="rz%d" % i)
                for n in ("sc", "r4", "r2", "bt", "nd", "c", "rc", "al"):
                    s[n] = keep.tile([P, 1], F32, name="%s%d" % (n, i))
                st[i] = s
            return st[i]

        def mm_p(i, j):
            z, b = take()
            for k in range(2):
                nc.tensor.matmul_mx(
                    out=z[:],
                    lhsT=hpc[i][:, P * k : P * (k + 1)].bitcast(FP8X4),
                    lhsT_scale=hps[i][:, P * k : P * (k + 1)],
                    rhs=wp_t[j][:, k, :].bitcast(FP8X4),
                    rhs_scale=p_sc[4 * k : P, BANK * j : BANK * (j + 1)],
                    start=(k == 0),
                    stop=(k == 1),
                )
            state(i)["z"][P_SIDE, j] = (z, b)

        def mm_q(i, j):
            z, b = take()
            nc.tensor.matmul_mx(
                out=z[:],
                lhsT=hqc[i][:].bitcast(FP8X4),
                lhsT_scale=hqs[i][:],
                rhs=wq_t[j][:, 0, :].bitcast(FP8X4),
                rhs_scale=q_sc[:, BANK * j : BANK * (j + 1)],
                start=True,
                stop=True,
            )
            state(i)["z"][Q_SIDE, j] = (z, b)

        def vmax(i, side, j):
            s = st[i]
            c = BLOCKS * side + j
            nc.vector.tensor_reduce(out=s["mx"][:, c : c + 1], in_=s["z"][side, j][0][:], axis=AX.X, op=ALU.max)

        def vmax_all(i, side):
            s = st[i]
            nc.vector.tensor_reduce(
                out=s["nm"][:, side : side + 1],
                in_=s["mx"][:, BLOCKS * side : BLOCKS * (side + 1)],
                axis=AX.X,
                op=ALU.max,
                negate=True,
            )

        def zcopy(i, side, j):
            s = st[i]
            if ("zb", side) not in s:
                s["zb", side] = work.tile([P, V], BF16, name="zb", align_bytes=64)
                s["zm", side] = work.tile([P, V // 2], BF16, name="zm", align_bytes=64)
            nc.scalar.copy(out=s["zb", side][:, BANK * j : BANK * (j + 1)], in_=s["z"][side, j][0][:])

        def fold(i, side, step):
            s = st[i]
            src, dst = (s["zb", side], s["zm", side]) if step % 2 == 0 else (s["zm", side], s["zb", side])
            w = V >> (step + 1)
            nc.vector.tensor_tensor(out=dst[:, 0:w], in0=src[:, 0:w], in1=src[:, w : 2 * w], op=ALU.max)

        def fold_end(i, side, step):
            s = st[i]
            src = s["zb", side] if step % 2 == 0 else s["zm", side]
            nc.vector.tensor_reduce(
                out=s["nm"][:, side : side + 1], in_=src[:, 0 : V >> step], axis=AX.X, op=ALU.max, negate=True
            )

        def exps(i, side, j):
            s = st[i]
            z, b = s["z"][side, j]
            c = BLOCKS * side + j
            nc.scalar.activation(
                out=s["exp"][side][:, BANK * j : BANK * (j + 1)].rearrange("p (u q e) -> p u q e", u=2, e=2),
                in_=upe(z[:]),
                func=ACT.Exp,
                bias=s["nm"][:, side : side + 1],
                scale=1.0,
                accum_out=s["zs"][:, c : c + 1],
            )
            give(b)

        def sums(i):
            s = st[i]
            nc.vector.tensor_reduce(
                out=s["zt"][:], in_=s["zs"][:].rearrange("p (a j) -> p a j", a=2), axis=AX.X, op=ALU.add
            )

        def inv_sums(i):
            s = st[i]
            nc.vector.reciprocal(out=s["rz"][:], in_=s["zt"][:])
            nc.scalar.activation(out=s["r4"][:], in_=s["rz"][:, P_SIDE : P_SIDE + 1], func=ACT.Copy, scale=0.25)
            nc.scalar.activation(out=s["r2"][:], in_=s["rz"][:, P_SIDE : P_SIDE + 1], func=ACT.Copy, scale=-0.5)

        def ratio(i):
            s = st[i]
            nc.vector.tensor_scalar(
                out=s["sc"][:],
                in0=s["zt"][:, P_SIDE : P_SIDE + 1],
                scalar1=2.0,
                scalar2=s["rz"][:, Q_SIDE : Q_SIDE + 1],
                op0=ALU.mult,
                op1=ALU.mult,
            )

        def vmin(i):
            s = st[i]
            s["m"] = work.tile([P, V], F32, name="m", align_bytes=64)
            s["a"] = work.tile([P, V], BF16, name="a", align_bytes=64)
            nc.vector.scalar_tensor_tensor(
                out=s["m"][:],
                in0=s["exp"][Q_SIDE][:],
                scalar=s["sc"][:, 0:1],
                in1=s["exp"][P_SIDE][:],
                op0=ALU.mult,
                op1=ALU.min,
                accum_out=s["bt"][:, 0:1],
            )

        def small_nd(i):
            s = st[i]
            nc.vector.tensor_scalar(
                out=s["nd"][:], in0=s["bt"][:], scalar1=s["r4"][:, 0:1], scalar2=-1.0, op0=ALU.mult, op1=ALU.add
            )

        def small_c(i):
            s = st[i]
            nc.vector.tensor_scalar(
                out=s["c"][:], in0=s["bt"][:], scalar1=s["r2"][:, 0:1], scalar2=1.0, op0=ALU.mult, op1=ALU.add
            )

        def small_rc(i):
            s = st[i]
            nc.vector.reciprocal(out=s["rc"][:], in_=s["c"][:])

        def small_al(i):
            s = st[i]
            nc.vector.tensor_scalar(
                out=s["al"][:],
                in0=s["rc"][:],
                scalar1=s["rc"][:, 0:1],
                scalar2=s["rz"][:, P_SIDE : P_SIDE + 1],
                op0=ALU.mult,
                op1=ALU.mult,
            )

        def vsub(i, lo, hi):
            s = st[i]
            nc.vector.scalar_tensor_tensor(
                out=s["m"][:, lo:hi],
                in0=s["m"][:, lo:hi],
                scalar=s["nd"][:, 0:1],
                in1=s["exp"][P_SIDE][:, lo:hi],
                op0=ALU.mult,
                op1=ALU.add,
            )

        def vgain(i, lo, hi):
            s = st[i]
            nc.vector.scalar_tensor_tensor(
                out=s["a"][:, lo:hi],
                in0=s["m"][:, lo:hi],
                scalar=s["al"][:, 0:1],
                in1=g_sb[:, lo:hi],
                op0=ALU.mult,
                op1=ALU.mult,
            )

        def diags(i):
            s = st[i]
            s["d1"] = work.tile([P, P], F32, name="d1", align_bytes=64)
            s["d2"] = work.tile([P, P], F32, name="d2", align_bytes=64)
            nc.scalar.activation(out=s["d1"][:], in_=ident[:], func=ACT.Copy, scale=s["al"][:, 0:1])
            nc.scalar.activation(out=s["d2"][:], in_=s["d1"][:], func=ACT.Copy, scale=s["nd"][:, 0:1])

        def mm_sub(i, k):
            s = st[i]
            t, b = take()
            s["r", k] = (t, b)
            cols = slice(BANK * k, BANK * (k + 1))
            nc.tensor.matmul(t[:], lhsT=s["d1"][:], rhs=s["exp"][P_SIDE][:, cols], start=True, stop=False)
            nc.tensor.matmul(t[:], lhsT=s["d2"][:], rhs=s["m"][:, cols], start=False, stop=True)

        def vgain_t(i, k):
            s = st[i]
            t, b = s["r", k]
            cols = slice(BANK * k, BANK * (k + 1))
            nc.vector.tensor_tensor(out=s["a"][:, cols], in0=t[:], in1=g_sb[:, cols], op=ALU.mult)
            give(b)

        def a_turn(i, k0, nk):
            s = st[i]
            if "ga" not in s:
                s["ga"] = work.tile([P, V], BF16, name="ga", align_bytes=64)
                s["ac"] = work.tile([P, BANK], U32, name="ac", align_bytes=64)
                s["as"] = work.tile([P, BANK], U8, name="as", align_bytes=64)
            t, b = take()
            words = s["a"][:].bitcast(F32)
            for k in range(nk):
                for u in range(2):
                    c = (2 * k + u) * P
                    w = 256 * (k0 + k) + P * u
                    nc.tensor.transpose(t[:, c : c + P], words[:, w : w + P], ident[:])
            nc.scalar.copy(
                out=as_words(s["ga"][:, BANK * k0 : BANK * (k0 + nk)], nk), in_=interleaved(t[:, 0 : 256 * nk], nk)
            )
            give(b)

        def a_quant(i, k0, nk):
            s = st[i]
            nc.vector.quantize_mx(
                out=s["ac"][:, P * k0 : P * (k0 + nk)].bitcast(FP8X4),
                scales=s["as"][:, P * k0 : P * (k0 + nk)],
                in_=s["ga"][:, BANK * k0 : BANK * (k0 + nk)],
            )

        def mm_out(i, k):
            s = st[i]
            if "o" not in s:
                s["o"] = [take(), take()]
            for h in range(2):
                nc.tensor.matmul_mx(
                    out=s["o"][h][0][:],
                    lhsT=s["ac"][:, P * k : P * (k + 1)].bitcast(FP8X4),
                    lhsT_scale=s["as"][:, P * k : P * (k + 1)],
                    rhs=e_t[k][:, BANK * h : BANK * (h + 1)].bitcast(FP8X4),
                    rhs_scale=e_sc[4 * k : P, BANK * h : BANK * (h + 1)],
                    start=(k == 0),
                    stop=(k == V // K_PASS - 1),
                )

        ps = keep.tile([P, 2, N], U8, name="ps", align_bytes=256)

        def read_out(i, h):
            s = st[i]
            if "of" not in s:
                s["of"] = work.tile([P, E], F32, name="of", align_bytes=64)
                s["ob"] = work.tile([P, E], BF16, name="ob", align_bytes=64)
                s["pc"] = work.tile([P, 2, P], U32, name="pc", align_bytes=64)
                s["go"] = work.tile([P, 2 * BANK], BF16, name="go", align_bytes=64)
                s["left"] = {0: 2, 1: 2}
            s["left"][h] -= 1
            if s["left"][h] == 0:
                give(s["o"][h][1])
            return s["o"][h][0]

        def evac_b(i, h, copy):
            o = read_out(i, h)
            copy(
                out=st[i]["ob"][:, BANK * h : BANK * (h + 1)].rearrange("p (u q e) -> p u q e", u=2, e=2), in_=upe(o[:])
            )

        def evac_f(i, h, copy):
            o = read_out(i, h)
            copy(out=st[i]["of"][:, BANK * h : BANK * (h + 1)], in_=o[:])

        def store_f(i):
            nc.sync.dma_start(out=out[P * i : P * (i + 1), :], in_=st[i]["of"][:])

        def store_f_half(i, h, queue):
            cols = slice(BANK * h, BANK * (h + 1))
            queue.dma_start(out=out[P * i : P * (i + 1), cols], in_=st[i]["of"][:, cols])

        def o_turn(i, k0, nk, copy):
            s = st[i]
            t, b = take()
            words = s["ob"][:].bitcast(F32)
            for c in range(2 * nk):
                w = 256 * k0 + P * c
                nc.tensor.transpose(t[:, P * c : P * (c + 1)], words[:, w : w + P], ident[:])
            copy(out=as_words(s["go"][:, BANK * k0 : BANK * (k0 + nk)], nk), in_=interleaved(t[:, 0 : 256 * nk], nk))
            give(b)

        def o_quant(i, k):
            s = st[i]
            nc.vector.quantize_mx(
                out=s["pc"][:, k, :].bitcast(FP8X4),
                scales=ps[:, k, P * i : P * (i + 1)],
                in_=s["go"][:, BANK * k : BANK * (k + 1)],
            )

        def store_codes(i):
            nc.sync.dma_start(
                out=out_words.rearrange("g p m t -> p g (m t)")[:, :, 4 * P * i : 4 * P * (i + 1)].bitcast(I32),
                in_=st[i]["pc"][:].bitcast(I32),
            )

        def store_scales():
            rows = ps[:].rearrange("p g m -> p (g m)").bitcast(I32)
            for quad in range(QUADRANTS):
                nc.sync.dma_start(
                    out=out_scales.bitcast(I32)[:, 4 * quad : 4 * quad + 4, :].rearrange("g r m -> r g m"),
                    in_=rows[32 * quad : 32 * quad + 4, :].rearrange("r (g m) -> r g m", g=2),
                )

        hq_turn(0)
        hq_turn(1)
        hp_turn(0)
        hq_quant(0)
        hp_quant(0)
        for j in range(4):
            mm_q(0, j)
        hq_turn(2)
        for j in range(4):
            mm_p(0, j)
        for j in range(4):
            vmax(0, Q_SIDE, j)
        hq_quant(1)
        vmax_all(0, Q_SIDE)
        hq_quant(2)
        for j in range(4):
            vmax(0, P_SIDE, j)
        for j in range(4):
            exps(0, Q_SIDE, j)
        hp_turn(1)
        for j in range(4):
            mm_q(1, j)
        vmax_all(0, P_SIDE)
        for j in range(2):
            vmax(1, Q_SIDE, j)
        for j in range(4):
            exps(0, P_SIDE, j)
        hp_turn(2)
        hp_quant(1)
        for j in range(2, 4):
            vmax(1, Q_SIDE, j)
        for j in range(4):
            mm_p(1, j)
        vmax(1, P_SIDE, 0)
        vmax_all(1, Q_SIDE)
        for j in range(4):
            exps(1, Q_SIDE, j)
        sums(0)
        for j in range(1, 3):
            vmax(1, P_SIDE, j)
        inv_sums(0)
        vmax(1, P_SIDE, 3)
        ratio(0)
        hq_turn(3)
        hp_quant(2)
        hp_turn(3)
        vmax_all(1, P_SIDE)
        for j in range(4):
            mm_p(2, j)
        vmin(0)
        vmax(2, P_SIDE, 0)
        small_nd(0)
        small_c(0)
        for j in range(1, 4):
            vmax(2, P_SIDE, j)
        small_rc(0)
        vsub(0, 0, 1536)
        for j in range(4):
            exps(1, P_SIDE, j)
        for j in range(4):
            g_turn(j)
        sums(1)
        for j in range(4):
            mm_q(2, j)
        small_al(0)
        for j in range(4):
            zcopy(2, Q_SIDE, j)
        vmax_all(2, P_SIDE)
        hp_quant(3)
        vgain(0, 0, 1536)
        fold(2, Q_SIDE, 0)
        for j in range(4):
            exps(2, P_SIDE, j)
        hq_quant(3)
        inv_sums(1)
        diags(0)
        for step in range(1, 3):
            fold(2, Q_SIDE, step)
        for j in range(3):
            mm_p(3, j)
        ratio(1)
        fold_end(2, Q_SIDE, 3)
        for j in range(4):
            exps(2, Q_SIDE, j)
        vmin(1)
        for j in range(2):
            vmax(3, P_SIDE, j)
        sums(2)
        mm_sub(0, 3)
        vgain_t(0, 3)
        a_turn(0, 0, 2)
        inv_sums(2)
        mm_p(3, 3)
        vmax(3, P_SIDE, 2)
        small_c(1)
        ratio(2)
        vmax(3, P_SIDE, 3)
        a_turn(0, 2, 2)
        for j in range(4):
            mm_q(3, j)
        small_rc(1)
        for j in range(4):
            zcopy(3, Q_SIDE, j)
        vmin(2)
        vmax_all(3, P_SIDE)
        fold(3, Q_SIDE, 0)
        a_quant(0, 0, 4)
        fold(3, Q_SIDE, 1)
        small_al(1)
        small_nd(1)
        small_nd(2)
        for j in range(4):
            exps(3, P_SIDE, j)
        small_c(2)
        fold(3, Q_SIDE, 2)
        vsub(1, 0, 1536)
        fold_end(3, Q_SIDE, 3)
        small_rc(2)
        diags(1)
        for k in range(4):
            mm_out(0, k)
        vgain(1, 0, 1536)
        small_al(2)
        for j in range(4):
            exps(3, Q_SIDE, j)
        mm_sub(1, 3)
        vsub(2, 0, 1024)
        diags(2)
        a_turn(1, 0, 2)
        sums(3)
        evac_f(0, 1, nc.scalar.copy)
        evac_b(0, 0, nc.scalar.copy)
        vgain_t(1, 3)
        evac_b(0, 1, nc.scalar.copy)
        inv_sums(3)
        vgain(2, 0, 1024)
        mm_sub(2, 2)
        a_turn(1, 2, 2)
        a_turn(2, 0, 2)
        mm_sub(2, 3)
        ratio(3)
        a_quant(1, 0, 2)
        evac_f(0, 0, nc.scalar.copy)
        vmin(3)
        a_quant(2, 0, 2)
        small_c(3)
        a_quant(1, 2, 2)
        store_f(0)
        o_turn(0, 0, 2, nc.scalar.copy)
        small_rc(3)
        small_nd(3)
        for k in range(2):
            mm_out(1, k)
        for k in range(2, 4):
            vgain_t(2, k)
        vsub(3, 0, 2048)
        a_turn(2, 2, 2)
        small_al(3)
        for k in range(2, 4):
            mm_out(1, k)
        evac_b(1, 0, nc.scalar.copy)
        a_quant(2, 2, 2)
        for k in range(3):
            mm_out(2, k)
        for k in range(4):
            vgain(3, BANK * k, BANK * (k + 1))
        evac_f(1, 0, nc.scalar.copy)
        evac_b(1, 1, nc.scalar.copy)
        evac_f(1, 1, nc.scalar.copy)
        a_turn(3, 0, 1)
        o_turn(1, 0, 2, nc.scalar.copy)
        a_turn(3, 1, 1)
        store_f(1)
        mm_out(2, 3)
        a_turn(3, 2, 1)
        a_quant(3, 0, 1)
        for k in range(2):
            o_quant(1, k)
        evac_f(2, 1, nc.scalar.copy)
        a_quant(3, 1, 1)
        for k in range(2):
            o_quant(0, k)
        a_quant(3, 2, 1)
        store_codes(1)
        store_codes(0)
        a_turn(3, 3, 1)
        for h in range(2):
            evac_b(2, h, nc.scalar.copy)
        a_quant(3, 3, 1)
        evac_f(2, 0, nc.vector.tensor_copy)
        for k in range(4):
            mm_out(3, k)
        evac_b(3, 1, nc.scalar.copy)
        evac_b(3, 0, nc.vector.tensor_copy)
        evac_f(3, 0, nc.vector.tensor_copy)
        o_turn(2, 0, 2, nc.scalar.copy)
        store_f(2)
        o_turn(3, 0, 1, nc.vector.tensor_copy)
        store_f_half(3, 0, nc.sync)
        for k in range(2):
            o_quant(2, k)
        store_codes(2)
        o_turn(3, 1, 1, nc.scalar.copy)
        for k in range(2):
            o_quant(3, k)
        evac_f(3, 1, nc.scalar.copy)
        store_codes(3)
        store_f_half(3, 1, nc.scalar)
        store_scales()
